import numpy as np, ml_dtypes
CORES = [10,34,74,98]
N = 4
BF = ml_dtypes.bfloat16
L, S, ST, GENS, K = 256, 8, 5, 2, 64
GW, XW = S * L, 16 * L
def parts(rng):
    g = rng.integers(0, XW, (N, 8, 16, GW)); h = rng.integers(0, GW, (N, 8, 16, GW)); x = rng.integers(0, 256, (N, 8, 16, XW))
    return g, h, x, rng.integers(0, 256, (N, 8, 16, L)), rng.integers(800, 1151, (N, 8))
def pack(g, h, x, a, t):
    return {"gn": np.ascontiguousarray(g.reshape(N, 128, GW)).astype(np.int32), "nb": np.ascontiguousarray(h.reshape(N, 128, GW)).astype(np.int32),
            "x": x.reshape(N, 128, XW).astype(np.float32).astype(BF), "th": np.repeat(t, 16, axis=1).reshape(N, 128, 1).astype(np.int32), "a0": a.reshape(N, 128, L).astype(np.float32).astype(BF)}
def setup_inputs(rng):
    return pack(*parts(rng))
def uneven(rng, n):
    v = np.floor(256 * rng.random((N, 8, 16, n)) * np.exp2(-rng.integers(0, 8, (N, 8, 1, n)).astype(np.float64))).astype(np.int64)
    return np.where(rng.random((N, 8, 1, n)) < 0.5, 255 - v, v)
def setup_inputs_spread(rng):
    g = (XW * rng.random((N, 8, 16, GW)) ** 3).astype(np.int64); h = (GW * rng.random((N, 8, 16, GW)) ** 2).astype(np.int64)
    g[:, 1::2] = XW - 1 - g[:, 1::2]; h[:, :, ::2] = GW - 1 - h[:, :, ::2]
    t = np.argsort(rng.random((N, 8)), axis=1) * 510 + rng.integers(0, 510, (N, 8))
    return pack(g, h, uneven(rng, XW), uneven(rng, L), t)
def twoends(rng, n):
    return np.where(rng.random((N, 8, 1, n)) < 0.7, 255 * rng.integers(0, 2, (N, 8, 1, n)), 255 * rng.integers(0, 2, (N, 8, 16, n)))
def setup_inputs_ends(rng):
    g, h, x, a, t = parts(rng)
    g = np.where(rng.random(g.shape) < 0.8, (XW - 1) * rng.integers(0, 2, g.shape), g); h = np.where(rng.random(h.shape) < 0.8, (GW - 1) * rng.integers(0, 2, h.shape), h)
    x = twoends(rng, XW); a = twoends(rng, L); x[..., 0] = 0; x[..., XW - 1] = 255
    for q in range(N): t[q, :7] = rng.permutation(np.array([0, 0, 4080, 4080, 4080, 2294, 2294]))
    t[:, 7] = 0
    for i in (0, 1, L - 2, L - 1):
        g[:, 7, 0, S * i] = XW - 1; h[:, 7, :, S * i] = GW - 1; a[:, 7, :, i] = 0
    g[:, 7, :15, GW - 1] = XW - 1; g[:, 7, 15, GW - 1] = 0
    return pack(g, h, x, a, t)
def setup_inputs_corners(rng):
    g, h, x, a, t = parts(rng); o = rng.permutation(8); t[:, o[0]] = 0; t[:, o[1]] = 4080
    for q in range(N):
        w = rng.permutation(o[2:])
        h[q, w[0]] = np.arange(GW); h[q, w[1]] = (GW - 1) * rng.integers(0, 2, (16, GW)); h[q, w[2]] = np.roll(np.arange(GW), -1)
        g[q, w[3]] = (XW - 1) * rng.integers(0, 2, (16, GW))
        b = w[4]; t[q, b] = 0; x[q, b, :, XW - 1] = 255; g[q, b, 15] = XW - 1
        i = rng.permutation(L)[:L // 2]; a[q, b][:, i] = x[q, b][:, g[q, b, 0, S * i]]
        x[q, w[5]] = 255 * rng.integers(0, 2, (16, XW))
    return pack(g, h, x, a, t)
def setup_inputs_ties(rng):
    g, h, x, a, t = parts(rng)
    x = 8 * rng.integers(0, 32, (N, 8, 1, XW)) + ((np.arange(16)[:, None] == rng.integers(0, 16, (N, 8, 1, XW))) & (rng.random((N, 8, 1, XW)) < 0.5))
    a = 8 * rng.integers(0, 32, (N, 8, 1, L)) + np.zeros((16, 1), np.int64)
    h[:, ::2] = h[:, ::2, :1]
    return pack(g, h, x, a, 16 * (8 * rng.integers(0, 6, (N, 8)) + 1))
def setup_inputs_counts(rng):
    g, h, x, a, t = parts(rng); q = rng.permutation(N); o = rng.permutation(8); w = int(o[0])
    t[q[0]] = 0; t[q[1]] = 4080; t[q[2]] = 4080; t[q[2], o[1:4]] = 0; t[q[3]] = 0
    if N > 4: t[q[4]] = 1170
    if N > 5: t[q[5], o[1:5]] = 0
    t[:, w] = 0; t[q[1], w] = 4080
    u = np.floor(rng.integers(2, 7, (N, 1, XW)) * rng.random((N, 16, XW))).astype(np.int64); u[:, 0] = 0
    x[:, w] = u; x[q[1], w] = 255 - u[q[1]]; x[q[1], w, 0] = 254
    a[:, w] = 255; a[:, w, 0] = 254
    for r, n in ((q[2], 64), (q[3], 8 * int(rng.integers(3, 5)) + int(rng.choice(np.array([2, 3, 5, 6]))))):
        i = rng.permutation(L)[:n]; a[r, w, 0, i] = 255; h[r, w, 0, S * i] = S * i
    return pack(g, h, x, a, t)
def check_inputs(d):
    bad = []
    for k, lo, hi in (("gn", 0, XW - 1), ("nb", 0, GW - 1), ("x", 0, 255), ("th", 0, 4080), ("a0", 0, 255)):
        v = np.asarray(d[k]).astype(np.float64)
        if not (np.min(v) >= lo and np.max(v) <= hi): bad.append("range of " + k)
        elif np.any(v != np.floor(v)): bad.append("whole numbers of " + k)
    v = np.asarray(d["th"]).reshape(-1, 16)
    if np.any(v != v[:, :1]): bad.append("equal rows of th in a group")
    return bad
def reference(gn, nb, x, th, a0):
    G = gn.astype(np.int64).reshape(N, 8, 16, GW); H = nb.astype(np.int64).reshape(N, 8, 16, GW); X = x.astype(np.float32).astype(np.int64).reshape(N, 8, 16, XW)
    lim = th.astype(np.int64).reshape(N, 8, 16)[:, :, :1]; a = a0.astype(np.float32).astype(np.int64).reshape(N, 8, 16, L)
    A = np.zeros(N, np.int64); lane = np.arange(L); kk = np.arange(16)[None, :, None]
    for gen in range(GENS):
        h = np.zeros((N, 8, L), np.int64) + S * lane; p = np.zeros((N, 8, L), np.int64); err = np.zeros((N, 8, L), np.int64)
        dau = G[..., ::S].copy()
        for t in range(ST):
            now = np.zeros(N, np.int64)
            for r in range(N):
                q = (r + t) % N; hr = h[r][:, None, :]; pr = p[r]
                n = np.take_along_axis(np.take_along_axis(G[q], hr, 2), pr[:, None, :], 1)[:, 0]
                T = np.abs(np.take_along_axis(X[q], n[:, None, :], 2) - a[r])
                ho = np.take_along_axis(H[q], hr, 2)
                at = ((pr[:, None, :] + kk) & 15) * GW + ho
                e = np.take_along_axis(G[q].reshape(8, 16 * GW), at.reshape(8, 16 * L), 1)
                v = np.take_along_axis(X[q], e[:, None, :], 2).reshape(8, 16, 16, L)
                D = np.add.reduce(np.abs(v + T[:, :, None, :] - 255), axis=1)
                ok = D <= (lim[q] + (A[q] & 63))[:, :, None]
                found = np.any(ok, axis=1); m = np.argmax(ok, axis=1)
                em = np.take_along_axis(e.reshape(8, 16, L), m[:, None, :], 1)[:, 0]; hm = np.take_along_axis(ho, m[:, None, :], 1)[:, 0]
                an = np.where(found[:, None, :], np.take_along_axis(X[q], em[:, None, :], 2), T)
                dau[r, :, t] = np.where(found, em, n); h[r] = np.where(found, hm, h[r]); p[r] = (pr + 1 + np.where(found, m, 0)) & 15
                err[r] = err[r] + np.where(found, 0, 1); now[q] = np.sum(np.where(found, 0, 1)); a[r] = an
                np.put_along_axis(X[q], (16 * lane + p[r])[:, None, :], an, 2)
            A = now
        order = np.argsort(err * L + lane, axis=2)
        best = np.take_along_axis(dau, order[:, :, None, :K], 3)
        come = np.where((np.arange(K) & 1) == 1, np.roll(best, 1, axis=0), best)
        worst = order[:, :, ::-1][:, :, :K]
        np.put_along_axis(G, (S * worst)[:, :, None, :], come, 3)
    return {"yg": G[..., ::S].reshape(N, 128, L).astype(np.float32), "ya": a.reshape(N, 128, L).astype(np.float32), "ys": np.add.reduce(X.reshape(N, 8, 16, L, 16), axis=4).reshape(N, 128, L).astype(np.float32)}

@@ -1,0 +1,484 @@
+from concourse.mybir import AluOpType, AxisListType, ActivationFunctionType
+OP = AluOpType
+AF = ActivationFunctionType
+N, GENS, ST, K = 4, 2, 5, 64
+L, GW, XW = 256, 2048, 4096
+ZC = 2048
+XB = XW + 16
+MAGIC = 12582913.0
+TAU = GENS * ST
+CUT = [(0, 128, (64, 64)), (128, 256, (64, 64))]
+NCH = len(CUT)
+TRA = 3
+DMAS = 20
+ORDER = """D0 RR1 TR0 SB1 OF1 NG1 E1.1 E1.0 X0.0 X0.1 NL1 D1 WW0 TR1 GO0 WW1 PK0 X1.0 X1.1 EE M10 GO1 PK1 M30 M20
+ RR0' M11 SB0' OF0' CO NG0' E0.0' M21 M31 E0.1' ST NL0' HI""".split()
+ROT = {"RR1": (11,), "TR0": (0, 3), "OF1": (1,), "D0": (5, 8, 4), "GO0": (2,), "PK0": (6, 7, 9, 10)}
+ROTA = (2, 4, 5, 6, 7, 8, 9, 10, 11)
+
+SCRATCH = {"dn": ("dram", [8, 19, GW], "int32")}
+for _n, _w, _d in (
+        ("gi", GW, "int32"), ("g4", 4 * GW, "float32"), ("n4", 4 * GW, "int32"), ("g16", GW, "float16"), ("xr", XB, "bfloat16"), ("zz", GW, "bfloat16"),
+        ("eg", 16 * L, "float16"), ("uu", 16 * L, "bfloat16"), ("ab", 16 * L, "float16"), ("tr", 16 * L, "bfloat16"),
+        ("rr", L, "float16"), ("sb", L, "float16"), ("ww", L, "bfloat16"), ("m0", L, "bfloat16"), ("of", L, "uint16"), ("ng", L, "float16"),
+        ("nl", 16, "uint16"), ("nf", 16, "float32"), ("dd", L, "bfloat16"), ("tt", L, "bfloat16"), ("xl", L, "uint16"),
+        ("ok", L, "bfloat16"), ("ff", L, "float16"), ("qq", 3 * L, "float16"), ("yy", L, "bfloat16"), ("xo", 16, "uint16"), ("ti", 64, "float32"),
+        ("yi", 16, "int32"), ("li", 64, "int32"), ("zs", 16, "float32"), ("zr", 16, "float32"), ("zf", 16, "float32"),
+        ("lo", 64 * TAU, "uint16"), ("ln", 64 * TAU, "uint16"), ("lc", 64, "uint16"), ("ci", 16, "int32"), ("cs", 16, "uint16"), ("cb", 16, "float32"),
+        ("ao", L * TAU, "bfloat16"), ("an", L * TAU, "bfloat16"), ("ho", 32 * TAU, "float16"), ("hn", 32 * TAU, "float16"), ("hl", 96, "float16"), ("er", 16, "float32"),
+        ("ed", 6 * L, "float16"), ("og", L, "float32"), ("gm", L, "float32"), ("da", L, "float32"), ("sr", L, "float32"), ("rv", L, "float32"),
+        ("bi", 2 * K, "float32"), ("o16", L, "float16"), ("ind", L, "float16"), ("pre", L, "float16"), ("on", L, "float16"), ("x1", L, "float16"), ("x2", L, "float16"),
+        ("pl", 16, "uint16"), ("pr", 16, "uint16"), ("af", 1, "float32"), ("ai", 2, "int32"), ("lim", 1, "float32"), ("thi", 1, "int32"), ("thf", 1, "float32"),
+        ("jj", L, "int32"), ("jf", L, "float32"), ("jt", 128, "int32"), ("kk", 16, "int32"), ("kb", 16, "int32"), ("kf", 16, "float32"), ("wf", 16, "float32"),
+        ("pi", 4, "int32"), ("pf", 8, "float32"), ("u16", 16, "float32"), ("g8", 8, "float16"), ("tw", 16, "bfloat16"), ("ts", 16, "bfloat16"), ("tm", 16, "bfloat16"),
+        ("se", 2048, "float16"), ("ss", 2048, "float16"), ("idn", 128, "float16"), ("ib", 128, "bfloat16"), ("bo", 128, "float16"), ("bh", 128, "bfloat16"),
+        ("lt", 128, "float16"), ("l2", 128, "float16"), ("one", 128, "float16"), ("rt", 384, "float16"), ("r2", 384, "float16"), ("jr", 384, "int32"),
+        ("fo", 3 * L, "float32")):
+    SCRATCH[_n] = ("sbuf", [128, _w], _d)
+PSUM = ["pe0", "pe1", "pd0", "pd1", "pl0", "pl1", "pa", "pb"]
+for _n in PSUM:
+    SCRATCH[_n] = ("psum", [128, 512], "float32")
+SEMAPHORES = ["v", "a", "p", "gc", "loc", "b0", "b1"] + ["d%d" % i for i in range(DMAS)] + ["h%d" % i for i in range(TAU)]
+for _b in range(NCH):
+    SEMAPHORES += ["li%d_%d" % (_t, _b) for _t in range(TAU)] + ["ar%d_%d" % (_t, _b) for _t in range(TAU)]
+
+
+def rank_program(g, core, T, topo):
+    rank = T.rank_of(core)
+    if rank is None:
+        return
+    queues = {"v": g.vector, "a": g.scalar, "p": g.tensor, "g": g, "s": g.sync}
+    own = {"v": "v", "a": "a", "p": "p", "g": "gc"}
+    cnt = {"v": 0, "a": 0, "p": 0, "gc": 0}
+    known = {q: {} for q in queues}
+    clock = {}
+    wr, rd = {}, {}
+    nd = [0]
+    locs = [0]
+
+    def R(name, lo=0, hi=None):
+        return (name, lo, SCRATCH[name][1][-1] if hi is None else hi)
+
+    def need(q, reads, writes):
+        best = {}
+
+        def look(lists, rs):
+            for name, lo, hi in rs:
+                ps = name in PSUM
+                for l, h, q2, (s, n) in lists.get(name, ()):
+                    if (q2 != q if ps else (l < hi and lo < h)) and n > known[q].get(s, 0) and n > best.get(s, 0):
+                        best[s] = n
+        look(wr, reads + writes)
+        look(rd, writes + [r for r in reads if r[0] in PSUM])
+        for s in sorted(best):
+            n = best[s]
+            if n > known[q].get(s, 0):
+                queues[q].wait_ge(T.sem[s], n)
+                known[q][s] = n
+                for s2, n2 in clock.get((s, n), {}).items():
+                    if n2 > known[q].get(s2, 0):
+                        known[q][s2] = n2
+
+    def note(q, reads, writes, tok):
+        for name, lo, hi in writes:
+            for d in (wr, rd):
+                d[name] = [e for e in d.get(name, ()) if not (lo <= e[0] and e[1] <= hi)]
+            wr[name].append((lo, hi, q, tok))
+        for name, lo, hi in reads:
+            rd[name] = [e for e in rd.get(name, ()) if not (lo <= e[0] and e[1] <= hi and e[2] == q)] + [(lo, hi, q, tok)]
+
+    def op(q, fn, reads, writes):
+        need(q, reads, writes)
+        s = own[q]
+        fn(queues[q]).then_inc(T.sem[s], 1)
+        cnt[s] += 1
+        clock[(s, cnt[s])] = dict(known[q])
+        note(q, reads, writes, (s, cnt[s]))
+
+    def dma(out, src, reads, writes):
+        need("s", reads, writes)
+        s = "d%d" % nd[0]
+        nd[0] += 1
+        g.sync.dma_start(out, src).then_inc(T.sem[s], 16)
+        clock[(s, 16)] = dict(known["s"])
+        note(s, reads, writes, (s, 16))
+
+    def send(dst, name, lo, hi, to, lo2, sem):
+        need("g", [(name, lo, hi)], [])
+        rid, pid, _ = topo.addr(dst)
+        ne = len(topo.engines(core, dst))
+        g.remote_dma(T[to][:, lo2:lo2 + hi - lo], T[name][:, lo:hi], T.sem[sem], T.sem.loc, pid, rid, topo.mask(core, dst))
+        locs[0] += ne
+        note(sem, [], [(to, lo2, lo2 + hi - lo)], (sem, ne))
+
+    def X(r):
+        if len(r) == 1:
+            return T[r[0]][:], R(r[0])
+        if len(r) == 4:
+            return T[r[0]][:, r[1]:r[2]:r[3]], r[0:3]
+        return T[r[0]][:, r[1]:r[2]], r
+
+    def G(win, off):
+        return X(win)[0].indirect(X(off)[0]), [X(win)[1], X(off)[1]]
+
+    def side(r):
+        if len(r) == 2 and isinstance(r[0], tuple):
+            return G(*r)
+        a, i = X(r)
+        return a, [i]
+
+    def sc(s):
+        return (X(s)[0], [X(s)[1]]) if isinstance(s, tuple) else (s, [])
+
+    def ts(out, src, s1, op0, s2=None, op1=None, tag=None):
+        o, io = side(out)
+        a, ia = side(src)
+        c1, i1 = sc(s1)
+        c2, i2 = sc(s2)
+        w = [tag] if tag else io
+        if op1 is None:
+            op("v", lambda v: v.tensor_scalar(o, a, c1, None, op0), ia + i1, w)
+        else:
+            op("v", lambda v: v.tensor_scalar(o, a, c1, c2, op0, op1), ia + i1 + i2, w)
+
+    def tt(out, a, b, op0, more=()):
+        o, io = side(out)
+        x, ix = side(a)
+        y, iy = side(b)
+        op("v", lambda v: v.tensor_tensor(o, x, y, op0), ix + iy + list(more), io)
+
+    def cp(out, src):
+        o, io = side(out)
+        a, ia = side(src)
+        op("v", lambda v: v.tensor_copy(o, a), ia + (io[1:] if len(io) > 1 else []), io[:1])
+
+    def act(out, src, f, bias=0.0, scale=1.0, tag=None):
+        o, io = side(out)
+        a, ia = side(src)
+        b, ib = sc(bias)
+        w = [tag] if tag else io
+        op("a", lambda s: s.activation(o, a, f, bias=b, scale=scale), ia + ib, w)
+
+    def mm(out, lhsT, rhs, start=True, stop=True):
+        o, io = side(out)
+        a, ia = side(lhsT)
+        b, ib = side(rhs)
+        op("p", lambda t: t.matmul(o, a, b, start, stop), ia + ib, io)
+
+    nxt = T.cores[(rank + 1) % N]
+
+    H = GW // 2
+    dma(T.gi[:, 0:H], T.gn[:, 0:H], [], [R("gi", 0, H)])
+    dma(T.gi[:, H:GW], T.gn[:, H:GW], [], [R("gi", H, GW)])
+    dma(T.n4[:, 0:GW], T.nb[:], [], [R("n4", 0, GW)])
+    dma(T.thi[:], T.th[:], [], [R("thi")])
+    dma(T.an[:, 0:L], T.a0[:], [], [R("an", 0, L)])
+    dma(T.xr[:, 0:ZC], T.x[:, 0:ZC], [], [R("xr", 0, ZC)])
+    op("g", lambda q: q.iota(T.pi[:, 0:1], [[0, 1]], 0, 1), [], [R("pi", 0, 1)])
+    op("g", lambda q: q.iota(T.jj[:], [[1, L]], 0, 0), [], [R("jj")])
+    op("g", lambda q: q.iota(T.kk[:], [[0, 4], [-1, 4]], 16, 1), [], [R("kk")])
+    op("g", lambda q: q.iota(T.jr[:], [[4, 3], [32, 8], [1, 16]], 4, 0), [], [R("jr")])
+    op("v", lambda v: v.memset(T.xr[:, ZC:XB], 0.0), [], [R("xr", ZC, XB)])
+    dma(T.xr[:, ZC + 1:XW + 1], T.x[:, ZC:XW], [], [R("xr", ZC, XB)])
+    dma(T.dn[:, 3:19, :], T.nb[:], [], [("dn", 3, 19)])
+    for k in range(3):
+        dma(T.dn[:, k, :], T.nb[13 + k::16, :], [], [("dn", k, k + 1)])
+    for k in range(1, 4):
+        dma(T.n4[:, k * GW:(k + 1) * GW], T.dn[:, 3 - k:19 - k, :], [("dn", 3 - k, 19 - k)], [R("n4", k * GW, (k + 1) * GW)])
+    op("v", lambda v: v.memset(T.zz[:], 0.0), [], [R("zz")])
+    ts(("pi", 1, 2), ("pi", 0, 1), 15, OP.bitwise_and)
+    ts(("pi", 2, 3), ("pi", 0, 1), 4, OP.arith_shift_right)
+    cp(("pf", 0, 3), ("pi", 0, 3))
+    ROW, GRP = ("pf", 1, 2), ("pf", 2, 3)
+    cp(("jf",), ("jj",))
+    ts(("idn",), ("jf", 0, 128), ("pf", 0, 1), OP.is_equal)
+    ts(("jt",), ("jj", 0, 128), 4, OP.arith_shift_right)
+    ts(("bo",), ("jt",), GRP, OP.is_equal)
+    ts(("g8",), ("jf", 0, 8), GRP, OP.is_equal)
+    ts(("u16",), ("jf", 0, 16), ROW, OP.is_equal)
+    act(("ss",), ("zz",), AF.Copy)
+    for k in range(16):
+        act(("ss", k * 128 + k, (k + 1) * 128, 16), ("g8",), AF.Copy)
+    act(("se",), ("zz",), AF.Copy)
+    for k in range(16):
+        act(("se", k * 128 + k, (k + 1) * 128, 16), ("idn", k, 128, 16), AF.Copy)
+    ts(("pf", 3, 4), ROW, 8.0, OP.mult)
+    ts(("pf", 4, 5), ROW, 16.0, OP.mult)
+    ts(("pf", 5, 6), ROW, 1.0, OP.add, 2048.0, OP.mult)
+    ts(("pf", 6, 7), ROW, 5.0, OP.is_ge)
+    ts(("pf", 7, 8), GRP, 16.0, OP.mult, ("pf", 0, 1), OP.add)
+    ts(("zf",), ("jf", 0, 16), 128.0, OP.mult, ("pf", 3, 4), OP.add)
+    cp(("lc", 0, 16), ("zf",))
+    ts(("lc", 16, 32), ("zf",), 0.0, OP.mult)
+    ts(("cb",), ("jf", 0, 16), 256.0, OP.mult, ("pf", 4, 5), OP.add)
+    ts(("cb", 8, 16), ("cb", 8, 16), 1.0, OP.add)
+    ts(("kk",), ("kk",), 15, OP.bitwise_and)
+    op("v", lambda v: v.memset(T.wf[:], 16777216.0), [], [R("wf")])
+    for j in range(4):
+        ts(("kb",), ("kk",), j, OP.arith_shift_right, 1, OP.bitwise_and)
+        ts(("kf",), ("kb",), 2.0 ** -(1 << j) - 1.0, OP.mult, 1.0, OP.add)
+        tt(("wf",), ("wf",), ("kf",), OP.mult)
+    cp(("tw",), ("wf",))
+    ts(("kb",), ("jj", 0, 16), 2, OP.arith_shift_right)
+    ts(("ts",), ("kb",), 2048.0, OP.mult)
+    cp(("tm",), ("u16",))
+    ts(("bh",), ("bo",), 0.5, OP.mult)
+    for lo in range(0, GW, H):
+        ts(("g4", lo, lo + H), ("gi", lo, lo + H), 1.0 + 2.0 ** -12, OP.mult, MAGIC, OP.add)
+        act(("g4", lo, lo + H), ("g4", lo, lo + H), AF.Copy, bias=-(MAGIC + 2048.0))
+    ts(("thf",), ("thi",), 1.0, OP.add)
+    ts(("lim",), ("thf",), 16777216.0, OP.mult)
+
+    def late_constants():
+        ts(("rt",), ("jr",), ("pf", 7, 8), OP.is_equal)
+        ts(("r2",), ("jr",), -16.0, OP.add, ("pf", 7, 8), OP.is_equal)
+        tt(("rt",), ("rt",), ("r2",), OP.add)
+        cp(("g16",), ("g4", 0, GW))
+
+    def later_constants():
+        cp(("ib",), ("idn",))
+        ts(("one",), ("jf", 0, 128), 0.0, OP.is_ge)
+        ts(("on",), ("jf",), 0.0, OP.is_ge)
+        ts(("jt",), ("jj", 0, 128), 15, OP.bitwise_and)
+        ts(("l2",), ("jt",), ROW, OP.is_gt)
+        tt(("lt",), ("l2",), ("bo",), OP.mult)
+        cp(("og",), ("g4", 0, GW, 8))
+
+    def turn(n):
+        s, lo = 1 + n // 4, 512 * (n % 4)
+        bank = ("pa", "pd1")[n % 2]
+        mm((bank,), ("rt", (s - 1) * 128, s * 128), ("g16", lo, lo + 512))
+        out = ("g4", s * GW + lo, s * GW + lo + 512)
+        if n in ROTA:
+            act(out, (bank,), AF.Copy)
+        else:
+            cp(out, (bank,))
+
+    def turn_own():
+        cp(("o16",), ("og",))
+        for s in range(1, 4):
+            bank = ("pa", "pd1")[s % 2]
+            mm((bank, 0, L), ("rt", (s - 1) * 128, s * 128), ("o16",))
+            cp(("g4", s * GW, (s + 1) * GW, 8), (bank, 0, L))
+
+    def lst(tau, b, kind):
+        c0, c1 = CUT[b][0:2]
+        n = (c1 - c0) // 16
+        if tau % ST == 0:
+            lo = (0 if kind in (1, 3) else 16) + c0 // 16
+            return ("lc", lo, lo + n)
+        lo = 64 * tau + c0 // 4 + kind * n
+        return ("ln", lo, lo + n)
+
+    def run(tok, tau):
+        gen, t = divmod(tau, ST)
+        tok, _, js = tok.partition(".")
+        kind = tok.rstrip("0123456789") if tok[0] != "M" else tok[0:2]
+        b = int(tok[len(kind):]) if tok[len(kind):] else 0
+        c0, c1, subs = CUT[b]
+        n = c1 - c0
+        l0, l1 = c0 // 16, c1 // 16
+        lc = l1 - l0
+        pe, pd, pn = "pe%d" % (b % 2), "pd%d" % (b % 2), "pl%d" % (b % 2)
+        p0 = 8 * l0
+        gw = GW if t == 0 else 4 * GW
+        e0 = c0 + sum(subs[0:int(js)]) if js else 0
+        e1 = e0 + subs[int(js)] if js else 0
+        q = 3 * c0
+        sco = (pd, 256 + c0, 256 + c1)
+        le, lr, ls = [(pn, p0 + 256 + k * lc, p0 + 256 + (k + 1) * lc) for k in range(3)]
+        hv = ("ho", 32 * tau + l0, 32 * tau + l1)
+        hf = ("ho", 32 * tau + 16 + l0, 32 * tau + 16 + l1)
+        li = [("li", c0 // 4 + k * lc, c0 // 4 + (k + 1) * lc) for k in range(4)]
+        if kind == "RR":
+            cp(("rr", c0, c1), (("n4", 0, gw), lst(tau, b, 1)))
+        elif kind == "SB":
+            act(("sb", c0, c1), (("ts", 0, 16), lst(tau, b, 2)), AF.Copy)
+            mm(("pb", c0, c1), ("idn",), ("rr", c0, c1), True, False)
+            mm(("pb", c0, c1), ("idn",), ("sb", c0, c1), False, True)
+            mm(("pb", 256 + c0, 256 + c1), ("idn",), ("rr", c0, c1))
+            act(("m0", c0, c1), (("tm", 0, 16), lst(tau, b, 2)), AF.Copy)
+        elif kind == "OF":
+            cp(("of", c0, c1), ("pb", c0, c1))
+        elif kind == "NG":
+            tt(("ng", c0, c1), (("g4", 0, GW), lst(tau, b, 3)), ("m0", c0, c1), OP.mult)
+            for a in range(16):
+                mm((pn, p0, p0 + lc), ("ss", a * 128, a * 128 + 128), ("ng", c0 + a, c1, 16), a == 0, a == 15)
+        elif kind == "NL":
+            ts(("nl", l0, l1), (pn, p0, p0 + lc), 2048.0, OP.add)
+            act(("nf", l0, l1), (pn, p0, p0 + lc), AF.Copy)
+        elif kind == "WW":
+            act(("ww", c0, c1), (("tw", 0, 16), lst(tau, b, 2)), AF.Copy)
+            ts(("zr", l0, l1), lst(tau, b, 1), 2048.0, OP.add)
+            cp(("zs", l0, l1), lst(tau, b, 0))
+        elif kind == "E":
+            act(("eg", 16 * e0, 16 * e1), (("g4", 0, gw), ("of", e0, e1)), AF.Copy)
+            for s in range(16):
+                mm((pe, e0, e1), ("se", s * 128, s * 128 + 128), ("eg", 16 * e0 + s, 16 * e1, 16), s == 0, s == 15)
+        elif kind == "D":
+            an, ao = ("an", L * tau) if t or tau == 0 else ("ao", L * (tau - 1))
+            tt(("dd", c0, c1), (("xr",), ("nl", l0, l1)), (an, ao + c0, ao + c1), OP.subtract)
+            act(("tt", c0, c1), ("dd", c0, c1), AF.Abs)
+        elif kind == "TR":
+            for s in range(16):
+                o = ("tr", 16 * c0 + s, 16 * c1, 16)
+                if s < TRA:
+                    act(o, ("tt", c0, c1), AF.Copy, bias=-255.0, tag=("tr%d" % s, c0, c1))
+                else:
+                    ts(o, ("tt", c0, c1), -255.0, OP.add, tag=("tr%d" % s, c0, c1))
+        elif kind == "X":
+            ts(("xl", e0, e1), (pe, e0, e1), 2048.0, OP.add)
+            trs = [("tr%d" % s, e0, e1) for s in range(16)]
+            o = X(("uu", 16 * e0, 16 * e1))
+            x = G(("xr",), ("xl", e0, e1))
+            op("v", lambda v: v.tensor_tensor(o[0], x[0], T.tr[:, 16 * e0:16 * e1], OP.add), x[1] + trs, [o[1]])
+            act(("ab", 16 * e0, 16 * e1), ("uu", 16 * e0, 16 * e1), AF.Abs)
+            for s in range(16):
+                mm((pd, e0, e1), ("ss", s * 128, s * 128 + 128), ("ab", 16 * e0 + s, 16 * e1, 16), s == 0, s == 15)
+        elif kind == "GO":
+            act((pd, c0, c1), (pd, c0, c1), AF.Relu, bias=("lim",), scale=-16777216.0)
+            tt(("ok", c0, c1), (pd, c0, c1), ("ww", c0, c1), OP.min)
+            mm(sco, ("bh",), ("ok", c0, c1))
+        elif kind == "PK":
+            tt(("ff", c0, c1), ("ok", c0, c1), sco, OP.is_gt)
+            tt(("qq", q, q + n), ("ff", c0, c1), (pe, c0, c1), OP.mult)
+            tt(("qq", q + n, q + 2 * n), ("ff", c0, c1), ("pb", 256 + c0, 256 + c1), OP.mult)
+            ts(("qq", q + 2 * n, q + 3 * n), ("ff", c0, c1), ("pf", 5, 6), OP.mult)
+            for a in range(16):
+                mm((pn, p0 + 256, p0 + 256 + 3 * lc), ("ss", a * 128, a * 128 + 128), ("qq", q + a, q + 3 * n, 16), a == 0, a == 15)
+            tt(("yy", c0, c1), ("tt", c0, c1), sco, OP.subtract)
+        elif kind == "M1":
+            def ti(k):
+                return ("ti", 16 * k + l0, 16 * k + l1)
+            yi = ("yi", l0, l1)
+            ts(hf, ls, 0.0, OP.is_equal)
+            ts(("xo", l0, l1), le, 2048.0, OP.add)
+            tt(ti(0), ls, ("zs", l0, l1), OP.add)
+            tt(ti(1), hf, ("zr", l0, l1), OP.mult)
+            tt(ti(2), lr, ti(1), OP.add)
+            tt(yi, ti(0), ti(2), OP.add)
+            ts(li[2], yi, 11, OP.arith_shift_right, 15, OP.bitwise_and)
+            if t < ST - 1:
+                for k, m in ((1, 8191), (3, 2047), (0, 24576)):
+                    ts(li[k], yi, m, OP.bitwise_and)
+                o = 64 * tau + c0 // 4
+                cp(("lo", o, o + 4 * lc), ("li", c0 // 4, c0 // 4 + 4 * lc))
+                send(nxt, "lo", o, o + 4 * lc, "ln", o + 64, "li%d_%d" % (tau, b))
+        elif kind == "M2":
+            ao = L * tau
+            tt(("ao", ao + c0, ao + c1), (("xr",), ("xo", l0, l1)), ("yy", c0, c1), OP.max)
+            if t < ST - 1:
+                send(nxt, "ao", ao + c0, ao + c1, "an", ao + L + c0, "ar%d_%d" % (tau, b))
+        elif kind == "M3":
+            tt(("ci", l0, l1), li[2], ("cb", l0, l1), OP.add)
+            cp(("cs", l0, l1), ("ci", l0, l1))
+            t3 = ("ti", 48 + l0, 48 + l1)
+            tt(t3, hf, ("nf", l0, l1), OP.mult)
+            tt(hv, le, t3, OP.add)
+        elif kind == "ST":
+            cp((("xr",), ("cs",)), ("ao", L * tau, L * tau + L))
+        elif kind == "HI":
+            if t in (1, 2, 3):
+                send(T.cores[(rank - t) % N], "ho", 32 * tau, 32 * tau + 32, "hn", 32 * tau, "h%d" % tau)
+        elif kind == "CO":
+            if tau < TAU - 1:
+                mm(("pa", 0, 16), ("one",), ("ho", 32 * tau + 16, 32 * tau + 32))
+                op("v", lambda v: v.tensor_reduce(T.af[:], T.pa[:, 0:16], AxisListType.X, OP.add), [R("pa")], [R("af")])
+                cp(("ai", 0, 1), ("af",))
+                ts(("ai", 1, 2), ("ai", 0, 1), 63, OP.bitwise_and)
+                ts(("lim",), ("ai", 1, 2), ("thf",), OP.add, 16777216.0, OP.mult)
+        elif kind == "EE" and t == ST - 1:
+            early_end(gen)
+
+    def plane(gen, t):
+        return "hn" if t in (1, 2, 3) else "ho", 32 * (ST * gen + t)
+
+    def spread(p0, p1):
+        for a in range(16):
+            ts(("ed", p0 * L + a, p1 * L, 16), ("hl", p0 * 16, p1 * 16), ("u16", a, a + 1), OP.mult, tag=("ed%d" % a, p0 * L, p1 * L))
+
+    EDS = [("ed%d" % a, 0, 6 * L) for a in range(16)]
+
+    def early_end(gen):
+        for t in range(4):
+            b, o = plane(gen, t)
+            cp(("hl", 16 * t, 16 * t + 16), (b, o, o + 16))
+            if t == 0:
+                cp(("er",), (b, o + 16, o + 32))
+            else:
+                tt(("er",), ("er",), (b, o + 16, o + 32), OP.add)
+        spread(0, 4)
+        ts(("gm",), ("og",), ("pf", 6, 7), OP.mult)
+
+    def registers_and_sums():
+        cp(("fo", L, 2 * L), ("ao", L * (TAU - 1), L * TAU))
+        dma(T.ya[:], T.fo[:, L:2 * L], [R("fo", L, 2 * L)], [])
+        for h in range(2):
+            o = h * (ZC + 1)
+            for s in range(16):
+                mm(("pe0", 128 * h, 128 * h + 128), ("ib",), ("xr", o + s, o + ZC, 16), s == 0, s == 15)
+        cp(("fo", 2 * L, 3 * L), ("pe0", 0, L))
+        dma(T.ys[:], T.fo[:, 2 * L:3 * L], [R("fo", 2 * L, 3 * L)], [])
+
+    def end(gen):
+        b, o = plane(gen, 4)
+        tt(("hl", 80, 96), ("er",), (b, o + 16, o + 32), OP.add)
+        cp(("hl", 64, 80), (b, o, o + 16))
+        spread(4, 6)
+        need("p", EDS, [])
+        mm(("pa", 0, L), ("bo",), ("ed", 5 * L, 6 * L))
+        for t in range(5):
+            mm(("pb", 0, L), ("ss", t * 128, t * 128 + 128), ("ed", t * L, (t + 1) * L), t == 0, t == 4)
+        ts(("ind",), ("pa", 0, L), ROW, OP.is_equal)
+        op("v", lambda v: v.tensor_tensor_scan(T.pre[:], T.on[:], T.ind[:], 0.0, OP.mult, OP.add), [R("on"), R("ind")], [R("pre")])
+        mm(("pa", 300, 301), ("lt",), ("pre", L - 1, L))
+        tt(("da",), ("pb", 0, L), ("gm",), OP.add)
+        ts(("x1",), ("pre",), ("pa", 300, 301), OP.add, -1.0, OP.add)
+        tt(("x2",), ("x1",), ("ind",), OP.mult)
+        for a in range(16):
+            mm(("pa", 320, 336), ("ss", a * 128, a * 128 + 128), ("x2", a, L, 16), a == 0, a == 15)
+        cp(("pl",), ("pa", 320, 336))
+        cp((("sr",), ("pl",)), ("da",))
+        ob = K * gen
+        send(nxt, "sr", 0, K, "bi", ob, "b%d" % gen)
+        ts(("pr",), ("pa", 320, 336), -1.0, OP.mult, 255.0, OP.add)
+        cp((("rv",), ("pr",)), ("og",))
+        cp(("rv", 0, K, 2), ("sr", 0, K, 2))
+        if gen == GENS - 1:
+            registers_and_sums()
+        cp(("rv", 1, K, 2), ("bi", ob + 1, ob + K, 2))
+        cp(("og",), (("rv",), ("pr",)))
+
+    for tau in range(TAU):
+        gen, t = divmod(tau, ST)
+        if t == 0:
+            for tok in ORDER:
+                if tok[-1] == "'":
+                    run(tok[0:-1], tau)
+                    if tau == 0 and tok == "RR0'":
+                        late_constants()
+        if tau == ST:
+            turn_own()
+        for tok in ORDER:
+            if tok[-1] != "'":
+                run(tok, tau)
+                for n in ROT.get(tok, ()) if tau == 0 else ():
+                    turn(n)
+                if tau == 0 and tok == "X1.0":
+                    later_constants()
+            elif t < ST - 1:
+                run(tok[0:-1], tau + 1)
+        if t == ST - 1:
+            end(gen)
+            if gen < GENS - 1:
+                cp(("g4", 0, GW, 8), ("og",))
+
+    ts(("fo", 0, L), ("og",), 0.0, OP.is_le, 2047.0, OP.add)
+    tt(("fo", 0, L), ("fo", 0, L), ("og",), OP.add)
+    dma(T.yg[:], T.fo[:, 0:L], [R("fo", 0, L)], [])
+    for i in range(nd[0]):
+        if known["s"].get("d%d" % i, 0) < 16:
+            g.sync.wait_ge(T.sem["d%d" % i], 16)
+    g.wait_ge(T.sem.loc, locs[0])
+    for s in ("v", "a", "p", "gc"):
+        g.sync.wait_ge(T.sem[s], cnt[s])

@@ -9,29 +9,33 @@ MAGIC = 12582913.0
 TAU = GENS * ST
 CUT = [(0, 128, (64, 64)), (128, 256, (64, 64))]
 NCH = len(CUT)
-TRA = 3
-DMAS = 20
-ORDER = """D0 RR1 TR0 SB1 OF1 NG1 E1.1 E1.0 X0.0 X0.1 NL1 D1 WW0 TR1 GO0 WW1 PK0 X1.0 X1.1 EE M10 GO1 PK1 M30 M20
- RR0' M11 SB0' OF0' CO NG0' E0.0' M21 M31 E0.1' ST NL0' HI""".split()
-ROT = {"RR1": (11,), "TR0": (0, 3), "OF1": (1,), "D0": (5, 8, 4), "GO0": (2,), "PK0": (6, 7, 9, 10)}
-ROTA = (2, 4, 5, 6, 7, 8, 9, 10, 11)
+DMAS = 26
+ORDER = """D0 NG1 DA0 WW1 OF1 TR0 E1.0 NL1 D1 X0.0 DA1 E1.1 X0.1 TR1 AB0.0 AB0.1 WW0 X1.0 GO0 GV0 PK0 YY0 X1.1 PC0 AB1.0 M10 ML0
+ AB1.1 GO1 EE GV1 MC0 PK1 M30 M20 YY1 RR0' PC1 SB0' M11 OF0' ML1 NG0' M21 MC1 M31 ST CO E0.1' E0.0' HI NL0' RR1' SB1'""".split()
+FIRST = """LC WW1 RR0 SB0 NG0 OF0 RR1 RT SB1 GC E0.0 E0.1 Q1 Q0 Q3 Q8 Q5 Q2 Q7 WW0 Q10 NL0 OF1 Q11 NG1 D0 DA0 TR0 Q9 E1.0 NL1 D1
+ X0.0 X0.1 DA1 TR1 Q6 E1.1 AB0.0 AB0.1 X1.0 GO0 GV0 PK0 X1.1 Q4 PC0 AB1.0 EE M10 AB1.1 GO1 ML0 M30 MC0 YY0 GV1 M20 PK1 YY1
+ RR0' PC1 M11 SB0' OF0' ML1 MC1 CO NG0' M31 M21 ST E0.0' E0.1' RR1' SB1' HI NL0'""".split()
+ROTA = (0, 2, 3, 4, 8, 10, 11)
+TRQ = ["aaggggvvvvvvvvvv", "aagggggggvvvvvvv"]
+HFA, YYA = (1, 0), (1, 0)
 
-SCRATCH = {"dn": ("dram", [8, 19, GW], "int32")}
+SCRATCH = {}
 for _n, _w, _d in (
-        ("gi", GW, "int32"), ("g4", 4 * GW, "float32"), ("n4", 4 * GW, "int32"), ("g16", GW, "float16"), ("xr", XB, "bfloat16"), ("zz", GW, "bfloat16"),
-        ("eg", 16 * L, "float16"), ("uu", 16 * L, "bfloat16"), ("ab", 16 * L, "float16"), ("tr", 16 * L, "bfloat16"),
+        ("gi", GW, "int32"), ("g4", 4 * GW, "float32"), ("n4", 4 * GW, "int32"), ("g16", GW, "float16"), ("xr", XB, "bfloat16"), ("w1", GW, "bfloat16"),
+        ("eg", 16 * L, "float16"), ("uu", 16 * L, "float16"), ("ab", 16 * L, "float16"), ("tr", 16 * L, "bfloat16"),
         ("rr", L, "float16"), ("sb", L, "float16"), ("ww", L, "bfloat16"), ("m0", L, "bfloat16"), ("of", L, "uint16"), ("ng", L, "float16"),
         ("nl", 16, "uint16"), ("nf", 16, "float32"), ("dd", L, "bfloat16"), ("tt", L, "bfloat16"), ("xl", L, "uint16"),
         ("ok", L, "bfloat16"), ("ff", L, "float16"), ("qq", 3 * L, "float16"), ("yy", L, "bfloat16"), ("xo", 16, "uint16"), ("ti", 64, "float32"),
         ("yi", 16, "int32"), ("li", 64, "int32"), ("zs", 16, "float32"), ("zr", 16, "float32"), ("zf", 16, "float32"),
         ("lo", 64 * TAU, "uint16"), ("ln", 64 * TAU, "uint16"), ("lc", 64, "uint16"), ("ci", 16, "int32"), ("cs", 16, "uint16"), ("cb", 16, "float32"),
-        ("ao", L * TAU, "bfloat16"), ("an", L * TAU, "bfloat16"), ("ho", 32 * TAU, "float16"), ("hn", 32 * TAU, "float16"), ("hl", 96, "float16"), ("er", 16, "float32"),
-        ("ed", 6 * L, "float16"), ("og", L, "float32"), ("gm", L, "float32"), ("da", L, "float32"), ("sr", L, "float32"), ("rv", L, "float32"),
+        ("ao", L * TAU, "bfloat16"), ("an", L * TAU, "bfloat16"), ("ho", 32 * TAU, "float16"), ("hn", 32 * TAU, "float16"), ("hl", 80, "float16"), ("er", 16, "float32"),
+        ("ed", 5 * L, "float16"), ("eb", L, "float16"), ("nb2", L, "float16"), ("et", L, "float16"),
+        ("og", L, "float32"), ("gm", L, "float32"), ("da", L, "float32"), ("sr", L, "float32"), ("rv", L, "float32"),
         ("bi", 2 * K, "float32"), ("o16", L, "float16"), ("ind", L, "float16"), ("pre", L, "float16"), ("on", L, "float16"), ("x1", L, "float16"), ("x2", L, "float16"),
         ("pl", 16, "uint16"), ("pr", 16, "uint16"), ("af", 1, "float32"), ("ai", 2, "int32"), ("lim", 1, "float32"), ("thi", 1, "int32"), ("thf", 1, "float32"),
         ("jj", L, "int32"), ("jf", L, "float32"), ("jt", 128, "int32"), ("kk", 16, "int32"), ("kb", 16, "int32"), ("kf", 16, "float32"), ("wf", 16, "float32"),
-        ("pi", 4, "int32"), ("pf", 8, "float32"), ("u16", 16, "float32"), ("g8", 8, "float16"), ("tw", 16, "bfloat16"), ("ts", 16, "bfloat16"), ("tm", 16, "bfloat16"),
-        ("se", 2048, "float16"), ("ss", 2048, "float16"), ("idn", 128, "float16"), ("ib", 128, "bfloat16"), ("bo", 128, "float16"), ("bh", 128, "bfloat16"),
+        ("pi", 4, "int32"), ("pf", 8, "float32"), ("u16", 16, "float32"), ("tw", 16, "bfloat16"), ("ts", 16, "bfloat16"), ("tm", 16, "bfloat16"),
+        ("se", 2048, "float16"), ("ss", 2048, "float16"), ("idn", 128, "float16"), ("ib", 128, "bfloat16"), ("bo", 128, "float16"), ("bh", 128, "bfloat16"), ("bn", 128, "bfloat16"),
         ("lt", 128, "float16"), ("l2", 128, "float16"), ("one", 128, "float16"), ("rt", 384, "float16"), ("r2", 384, "float16"), ("jr", 384, "int32"),
         ("fo", 3 * L, "float32")):
     SCRATCH[_n] = ("sbuf", [128, _w], _d)
@@ -95,13 +99,20 @@ def rank_program(g, core, T, topo):
         clock[(s, cnt[s])] = dict(known[q])
         note(q, reads, writes, (s, cnt[s]))
 
-    def dma(out, src, reads, writes):
-        need("s", reads, writes)
-        s = "d%d" % nd[0]
-        nd[0] += 1
-        g.sync.dma_start(out, src).then_inc(T.sem[s], 16)
-        clock[(s, 16)] = dict(known["s"])
-        note(s, reads, writes, (s, 16))
+    def dma(pairs, reads, reg, out=False):
+        need("s", reads, [] if out else [reg])
+        toks = []
+        for o, src in pairs:
+            s = "d%d" % nd[0]
+            nd[0] += 1
+            g.sync.dma_start(o, src).then_inc(T.sem[s], 16)
+            clock[(s, 16)] = dict(known["s"])
+            toks.append((s, (s, 16)))
+        for s, tok in toks:
+            if len(pairs) > 1:
+                wr[reg[0]] = list(wr.get(reg[0], ())) + [reg[1:3] + (s, tok)]
+            else:
+                note(s, reads, [] if out else [reg], tok)
 
     def send(dst, name, lo, hi, to, lo2, sem):
         need("g", [(name, lo, hi)], [])
@@ -118,12 +129,9 @@ def rank_program(g, core, T, topo):
             return T[r[0]][:, r[1]:r[2]:r[3]], r[0:3]
         return T[r[0]][:, r[1]:r[2]], r
 
-    def G(win, off):
-        return X(win)[0].indirect(X(off)[0]), [X(win)[1], X(off)[1]]
-
     def side(r):
         if len(r) == 2 and isinstance(r[0], tuple):
-            return G(*r)
+            return X(r[0])[0].indirect(X(r[1])[0]), [X(r[0])[1], X(r[1])[1]]
         a, i = X(r)
         return a, [i]
 
@@ -147,17 +155,30 @@ def rank_program(g, core, T, topo):
         y, iy = side(b)
         op("v", lambda v: v.tensor_tensor(o, x, y, op0), ix + iy + list(more), io)
 
-    def cp(out, src):
+    def cp(out, src, tag=None):
         o, io = side(out)
         a, ia = side(src)
-        op("v", lambda v: v.tensor_copy(o, a), ia + (io[1:] if len(io) > 1 else []), io[:1])
+        op("v", lambda v: v.tensor_copy(o, a), ia + (io[1:] if len(io) > 1 else []), [tag] if tag else io[:1])
 
     def act(out, src, f, bias=0.0, scale=1.0, tag=None):
         o, io = side(out)
         a, ia = side(src)
         b, ib = sc(bias)
-        w = [tag] if tag else io
-        op("a", lambda s: s.activation(o, a, f, bias=b, scale=scale), ia + ib, w)
+        c, ic = sc(scale)
+        op("a", lambda s: s.activation(o, a, f, bias=b, scale=c), ia + ib + ic, [tag] if tag else io)
+
+    def sel(out, src, pattern, cmp, base, ch, tag=None):
+        o, io = side(out)
+        a, ia = side(src)
+        op("g", lambda q: q.affine_select(o, a, pattern, cmp, 0.0, base, ch), ia, [tag] if tag else io)
+
+    def iota(out, pattern, base, ch):
+        o, io = side(out)
+        op("g", lambda q: q.iota(o, pattern, base, ch), [], io)
+
+    def fill(out, c):
+        o, io = side(out)
+        op("v", lambda v: v.memset(o, c), [], io)
 
     def mm(out, lhsT, rhs, start=True, stop=True):
         o, io = side(out)
@@ -168,24 +189,27 @@ def rank_program(g, core, T, topo):
     nxt = T.cores[(rank + 1) % N]
 
     H = GW // 2
-    dma(T.gi[:, 0:H], T.gn[:, 0:H], [], [R("gi", 0, H)])
-    dma(T.gi[:, H:GW], T.gn[:, H:GW], [], [R("gi", H, GW)])
-    dma(T.n4[:, 0:GW], T.nb[:], [], [R("n4", 0, GW)])
-    dma(T.thi[:], T.th[:], [], [R("thi")])
-    dma(T.an[:, 0:L], T.a0[:], [], [R("an", 0, L)])
-    dma(T.xr[:, 0:ZC], T.x[:, 0:ZC], [], [R("xr", 0, ZC)])
-    op("g", lambda q: q.iota(T.pi[:, 0:1], [[0, 1]], 0, 1), [], [R("pi", 0, 1)])
-    op("g", lambda q: q.iota(T.jj[:], [[1, L]], 0, 0), [], [R("jj")])
-    op("g", lambda q: q.iota(T.kk[:], [[0, 4], [-1, 4]], 16, 1), [], [R("kk")])
-    op("g", lambda q: q.iota(T.jr[:], [[4, 3], [32, 8], [1, 16]], 4, 0), [], [R("jr")])
-    op("v", lambda v: v.memset(T.xr[:, ZC:XB], 0.0), [], [R("xr", ZC, XB)])
-    dma(T.xr[:, ZC + 1:XW + 1], T.x[:, ZC:XW], [], [R("xr", ZC, XB)])
-    dma(T.dn[:, 3:19, :], T.nb[:], [], [("dn", 3, 19)])
-    for k in range(3):
-        dma(T.dn[:, k, :], T.nb[13 + k::16, :], [], [("dn", k, k + 1)])
+    for lo in (0, H):
+        dma([(T.gi[:, lo:lo + H], T.gn[:, lo:lo + H])], [], R("gi", lo, lo + H))
+    dma([(T.n4[:, 0:GW], T.nb[:])], [], R("n4", 0, GW))
+    dma([(T.thi[:], T.th[:])], [], R("thi"))
+    dma([(T.an[:, 0:L], T.a0[:])], [], R("an", 0, L))
+    dma([(T.xr[:, 0:ZC], T.x[:, 0:ZC])], [], R("xr", 0, ZC))
+    iota(("pi", 0, 1), [[0, 1]], 0, 1)
+    iota(("jj",), [[1, L]], 0, 0)
+    iota(("kk",), [[0, 4], [-1, 4]], 16, 1)
+    fill(("w1",), 1.0)
+    fill(("xr", ZC, XB), 0.0)
+    dma([(T.xr[:, ZC + 1:XW + 1], T.x[:, ZC:XW])], [], R("xr", ZC, XB))
     for k in range(1, 4):
-        dma(T.n4[:, k * GW:(k + 1) * GW], T.dn[:, 3 - k:19 - k, :], [("dn", 3 - k, 19 - k)], [R("n4", k * GW, (k + 1) * GW)])
-    op("v", lambda v: v.memset(T.zz[:], 0.0), [], [R("zz")])
+        reg = R("n4", k * GW, (k + 1) * GW)
+        dma([(T.n4[k:128, reg[1]:reg[2]], T.nb[0:128 - k, :])], [], reg)
+        rows = [(T.n4[u::16, reg[1]:reg[2]], T.nb[16 - k + u::16, :]) for u in range(k)]
+        dma(rows, [], reg)
+    sel(("ss",), ("w1",), [[16384, 16], [-16, 8], [-16384, 16]], OP.is_ge, 0, 1)
+    sel(("ss",), ("ss",), [[-16384, 16], [16, 8], [16384, 16]], OP.is_ge, 15, -1)
+    sel(("se",), ("w1",), [[-1024, 16], [16, 8], [1025, 16]], OP.is_equal, 0, -1)
+    iota(("jr",), [[4, 3], [32, 8], [1, 16]], 4, 0)
     ts(("pi", 1, 2), ("pi", 0, 1), 15, OP.bitwise_and)
     ts(("pi", 2, 3), ("pi", 0, 1), 4, OP.arith_shift_right)
     cp(("pf", 0, 3), ("pi", 0, 3))
@@ -194,14 +218,7 @@ def rank_program(g, core, T, topo):
     ts(("idn",), ("jf", 0, 128), ("pf", 0, 1), OP.is_equal)
     ts(("jt",), ("jj", 0, 128), 4, OP.arith_shift_right)
     ts(("bo",), ("jt",), GRP, OP.is_equal)
-    ts(("g8",), ("jf", 0, 8), GRP, OP.is_equal)
     ts(("u16",), ("jf", 0, 16), ROW, OP.is_equal)
-    act(("ss",), ("zz",), AF.Copy)
-    for k in range(16):
-        act(("ss", k * 128 + k, (k + 1) * 128, 16), ("g8",), AF.Copy)
-    act(("se",), ("zz",), AF.Copy)
-    for k in range(16):
-        act(("se", k * 128 + k, (k + 1) * 128, 16), ("idn", k, 128, 16), AF.Copy)
     ts(("pf", 3, 4), ROW, 8.0, OP.mult)
     ts(("pf", 4, 5), ROW, 16.0, OP.mult)
     ts(("pf", 5, 6), ROW, 1.0, OP.add, 2048.0, OP.mult)
@@ -210,39 +227,39 @@ def rank_program(g, core, T, topo):
     ts(("zf",), ("jf", 0, 16), 128.0, OP.mult, ("pf", 3, 4), OP.add)
     cp(("lc", 0, 16), ("zf",))
     ts(("lc", 16, 32), ("zf",), 0.0, OP.mult)
-    ts(("cb",), ("jf", 0, 16), 256.0, OP.mult, ("pf", 4, 5), OP.add)
-    ts(("cb", 8, 16), ("cb", 8, 16), 1.0, OP.add)
-    ts(("kk",), ("kk",), 15, OP.bitwise_and)
-    op("v", lambda v: v.memset(T.wf[:], 16777216.0), [], [R("wf")])
-    for j in range(4):
-        ts(("kb",), ("kk",), j, OP.arith_shift_right, 1, OP.bitwise_and)
-        ts(("kf",), ("kb",), 2.0 ** -(1 << j) - 1.0, OP.mult, 1.0, OP.add)
-        tt(("wf",), ("wf",), ("kf",), OP.mult)
-    cp(("tw",), ("wf",))
     ts(("kb",), ("jj", 0, 16), 2, OP.arith_shift_right)
     ts(("ts",), ("kb",), 2048.0, OP.mult)
     cp(("tm",), ("u16",))
-    ts(("bh",), ("bo",), 0.5, OP.mult)
-    for lo in range(0, GW, H):
+    for lo in (0, H):
         ts(("g4", lo, lo + H), ("gi", lo, lo + H), 1.0 + 2.0 ** -12, OP.mult, MAGIC, OP.add)
         act(("g4", lo, lo + H), ("g4", lo, lo + H), AF.Copy, bias=-(MAGIC + 2048.0))
-    ts(("thf",), ("thi",), 1.0, OP.add)
-    ts(("lim",), ("thf",), 16777216.0, OP.mult)
 
-    def late_constants():
-        ts(("rt",), ("jr",), ("pf", 7, 8), OP.is_equal)
-        ts(("r2",), ("jr",), -16.0, OP.add, ("pf", 7, 8), OP.is_equal)
-        tt(("rt",), ("rt",), ("r2",), OP.add)
-        cp(("g16",), ("g4", 0, GW))
-
-    def later_constants():
+    def constants():
+        ts(("kk",), ("kk",), 15, OP.bitwise_and)
+        fill(("wf",), 16777216.0)
+        for j in range(4):
+            ts(("kb",), ("kk",), j, OP.arith_shift_right, 1, OP.bitwise_and)
+            ts(("kf",), ("kb",), 2.0 ** -(1 << j) - 1.0, OP.mult, 1.0, OP.add)
+            tt(("wf",), ("wf",), ("kf",), OP.mult)
+        cp(("tw",), ("wf",))
+        ts(("bh",), ("bo",), 0.5, OP.mult)
+        ts(("bn",), ("bo",), -0.5, OP.mult)
         cp(("ib",), ("idn",))
-        ts(("one",), ("jf", 0, 128), 0.0, OP.is_ge)
-        ts(("on",), ("jf",), 0.0, OP.is_ge)
+        ts(("cb",), ("jf", 0, 16), 256.0, OP.mult, ("pf", 4, 5), OP.add)
+        ts(("cb", 8, 16), ("cb", 8, 16), 1.0, OP.add)
+        cp(("one",), ("w1", 0, 128))
+        cp(("on",), ("w1", 0, L))
         ts(("jt",), ("jj", 0, 128), 15, OP.bitwise_and)
         ts(("l2",), ("jt",), ROW, OP.is_gt)
         tt(("lt",), ("l2",), ("bo",), OP.mult)
+        ts(("thf",), ("thi",), 1.0, OP.add)
+        ts(("lim",), ("thf",), 16777216.0, OP.mult)
         cp(("og",), ("g4", 0, GW, 8))
+
+    def turns():
+        ts(("rt",), ("jr",), ("pf", 7, 8), OP.is_equal)
+        ts(("r2",), ("jr",), -16.0, OP.add, ("pf", 7, 8), OP.is_equal)
+        tt(("rt",), ("rt",), ("r2",), OP.add)
 
     def turn(n):
         s, lo = 1 + n // 4, 512 * (n % 4)
@@ -259,7 +276,10 @@ def rank_program(g, core, T, topo):
         for s in range(1, 4):
             bank = ("pa", "pd1")[s % 2]
             mm((bank, 0, L), ("rt", (s - 1) * 128, s * 128), ("o16",))
-            cp(("g4", s * GW, (s + 1) * GW, 8), (bank, 0, L))
+            if s == 2:
+                act(("g4", s * GW, (s + 1) * GW, 8), (bank, 0, L), AF.Copy)
+            else:
+                cp(("g4", s * GW, (s + 1) * GW, 8), (bank, 0, L))
 
     def lst(tau, b, kind):
         c0, c1 = CUT[b][0:2]
@@ -280,16 +300,17 @@ def rank_program(g, core, T, topo):
         l0, l1 = c0 // 16, c1 // 16
         lc = l1 - l0
         pe, pd, pn = "pe%d" % (b % 2), "pd%d" % (b % 2), "pl%d" % (b % 2)
-        p0 = 8 * l0
         gw = GW if t == 0 else 4 * GW
         e0 = c0 + sum(subs[0:int(js)]) if js else 0
         e1 = e0 + subs[int(js)] if js else 0
         q = 3 * c0
         sco = (pd, 256 + c0, 256 + c1)
-        le, lr, ls = [(pn, p0 + 256 + k * lc, p0 + 256 + (k + 1) * lc) for k in range(3)]
+        le, lr, ls = [(pn, 64 + k * lc, 64 + (k + 1) * lc) for k in range(3)]
         hv = ("ho", 32 * tau + l0, 32 * tau + l1)
         hf = ("ho", 32 * tau + 16 + l0, 32 * tau + 16 + l1)
         li = [("li", c0 // 4 + k * lc, c0 // 4 + (k + 1) * lc) for k in range(4)]
+        yi = ("yi", l0, l1)
+        ti = [("ti", 16 * k + l0, 16 * k + l1) for k in range(4)]
         if kind == "RR":
             cp(("rr", c0, c1), (("n4", 0, gw), lst(tau, b, 1)))
         elif kind == "SB":
@@ -303,10 +324,10 @@ def rank_program(g, core, T, topo):
         elif kind == "NG":
             tt(("ng", c0, c1), (("g4", 0, GW), lst(tau, b, 3)), ("m0", c0, c1), OP.mult)
             for a in range(16):
-                mm((pn, p0, p0 + lc), ("ss", a * 128, a * 128 + 128), ("ng", c0 + a, c1, 16), a == 0, a == 15)
+                mm((pn, 0, lc), ("ss", a * 128, a * 128 + 128), ("ng", c0 + a, c1, 16), a == 0, a == 15)
         elif kind == "NL":
-            ts(("nl", l0, l1), (pn, p0, p0 + lc), 2048.0, OP.add)
-            act(("nf", l0, l1), (pn, p0, p0 + lc), AF.Copy)
+            ts(("nl", l0, l1), (pn, 0, lc), 2048.0, OP.add)
+            act(("nf", l0, l1), (pn, 0, lc), AF.Copy)
         elif kind == "WW":
             act(("ww", c0, c1), (("tw", 0, 16), lst(tau, b, 2)), AF.Copy)
             ts(("zr", l0, l1), lst(tau, b, 1), 2048.0, OP.add)
@@ -318,46 +339,58 @@ def rank_program(g, core, T, topo):
         elif kind == "D":
             an, ao = ("an", L * tau) if t or tau == 0 else ("ao", L * (tau - 1))
             tt(("dd", c0, c1), (("xr",), ("nl", l0, l1)), (an, ao + c0, ao + c1), OP.subtract)
+        elif kind == "DA":
             act(("tt", c0, c1), ("dd", c0, c1), AF.Abs)
         elif kind == "TR":
-            for s in range(16):
-                o = ("tr", 16 * c0 + s, 16 * c1, 16)
-                if s < TRA:
-                    act(o, ("tt", c0, c1), AF.Copy, bias=-255.0, tag=("tr%d" % s, c0, c1))
+            for s, w in enumerate(TRQ[b]):
+                o, tag = ("tr", 16 * c0 + s, 16 * c1, 16), ("tr%d" % s, c0, c1)
+                if w == "a":
+                    act(o, ("tt", c0, c1), AF.Copy, tag=tag)
+                elif w == "g":
+                    sel(o, ("tt", c0, c1), [[0, n]], OP.is_ge, 0, 0, tag=tag)
                 else:
-                    ts(o, ("tt", c0, c1), -255.0, OP.add, tag=("tr%d" % s, c0, c1))
+                    cp(o, ("tt", c0, c1), tag=tag)
         elif kind == "X":
             ts(("xl", e0, e1), (pe, e0, e1), 2048.0, OP.add)
-            trs = [("tr%d" % s, e0, e1) for s in range(16)]
-            o = X(("uu", 16 * e0, 16 * e1))
-            x = G(("xr",), ("xl", e0, e1))
-            op("v", lambda v: v.tensor_tensor(o[0], x[0], T.tr[:, 16 * e0:16 * e1], OP.add), x[1] + trs, [o[1]])
-            act(("ab", 16 * e0, 16 * e1), ("uu", 16 * e0, 16 * e1), AF.Abs)
+            tt(("uu", 16 * e0, 16 * e1), (("xr",), ("xl", e0, e1)), ("tr", 16 * e0, 16 * e1), OP.add, more=[("tr%d" % s, e0, e1) for s in range(16)])
+        elif kind == "AB":
+            act(("ab", 16 * e0, 16 * e1), ("uu", 16 * e0, 16 * e1), AF.Abs, bias=-255.0)
             for s in range(16):
                 mm((pd, e0, e1), ("ss", s * 128, s * 128 + 128), ("ab", 16 * e0 + s, 16 * e1, 16), s == 0, s == 15)
         elif kind == "GO":
             act((pd, c0, c1), (pd, c0, c1), AF.Relu, bias=("lim",), scale=-16777216.0)
+        elif kind == "GV":
             tt(("ok", c0, c1), (pd, c0, c1), ("ww", c0, c1), OP.min)
             mm(sco, ("bh",), ("ok", c0, c1))
         elif kind == "PK":
             tt(("ff", c0, c1), ("ok", c0, c1), sco, OP.is_gt)
             tt(("qq", q, q + n), ("ff", c0, c1), (pe, c0, c1), OP.mult)
             tt(("qq", q + n, q + 2 * n), ("ff", c0, c1), ("pb", 256 + c0, 256 + c1), OP.mult)
-            ts(("qq", q + 2 * n, q + 3 * n), ("ff", c0, c1), ("pf", 5, 6), OP.mult)
+            act(("qq", q + 2 * n, q + 3 * n), ("ff", c0, c1), AF.Copy, scale=("pf", 5, 6))
+        elif kind == "PC":
             for a in range(16):
-                mm((pn, p0 + 256, p0 + 256 + 3 * lc), ("ss", a * 128, a * 128 + 128), ("qq", q + a, q + 3 * n, 16), a == 0, a == 15)
-            tt(("yy", c0, c1), ("tt", c0, c1), sco, OP.subtract)
+                mm((pn, 64, 64 + 3 * lc), ("ss", a * 128, a * 128 + 128), ("qq", q + a, q + 3 * n, 16), a == 0, a == 15)
+        elif kind == "YY":
+            if t == ST - 1:
+                act(("nb2", c0, c1), sco, AF.Relu, bias=1.0, scale=-1.0)
+            if YYA[b]:
+                mm((pn, 384, 384 + n), ("ib",), ("tt", c0, c1), True, False)
+                mm((pn, 384, 384 + n), ("bn",), ("ok", c0, c1), False, True)
+                act(("yy", c0, c1), (pn, 384, 384 + n), AF.Relu)
+            else:
+                tt(("yy", c0, c1), ("tt", c0, c1), sco, OP.subtract)
         elif kind == "M1":
-            def ti(k):
-                return ("ti", 16 * k + l0, 16 * k + l1)
-            yi = ("yi", l0, l1)
-            ts(hf, ls, 0.0, OP.is_equal)
+            if HFA[b]:
+                act(hf, ls, AF.Relu, bias=1.0, scale=-1.0)
+            else:
+                ts(hf, ls, 0.0, OP.is_equal)
             ts(("xo", l0, l1), le, 2048.0, OP.add)
-            tt(ti(0), ls, ("zs", l0, l1), OP.add)
-            tt(ti(1), hf, ("zr", l0, l1), OP.mult)
-            tt(ti(2), lr, ti(1), OP.add)
-            tt(yi, ti(0), ti(2), OP.add)
+            tt(ti[0], ls, ("zs", l0, l1), OP.add)
+            tt(ti[1], hf, ("zr", l0, l1), OP.mult)
+            tt(ti[2], lr, ti[1], OP.add)
+            tt(yi, ti[0], ti[2], OP.add)
             ts(li[2], yi, 11, OP.arith_shift_right, 15, OP.bitwise_and)
+        elif kind == "ML":
             if t < ST - 1:
                 for k, m in ((1, 8191), (3, 2047), (0, 24576)):
                     ts(li[k], yi, m, OP.bitwise_and)
@@ -369,12 +402,12 @@ def rank_program(g, core, T, topo):
             tt(("ao", ao + c0, ao + c1), (("xr",), ("xo", l0, l1)), ("yy", c0, c1), OP.max)
             if t < ST - 1:
                 send(nxt, "ao", ao + c0, ao + c1, "an", ao + L + c0, "ar%d_%d" % (tau, b))
-        elif kind == "M3":
+        elif kind == "MC":
             tt(("ci", l0, l1), li[2], ("cb", l0, l1), OP.add)
             cp(("cs", l0, l1), ("ci", l0, l1))
-            t3 = ("ti", 48 + l0, 48 + l1)
-            tt(t3, hf, ("nf", l0, l1), OP.mult)
-            tt(hv, le, t3, OP.add)
+        elif kind == "M3":
+            tt(ti[3], hf, ("nf", l0, l1), OP.mult)
+            tt(hv, le, ti[3], OP.add)
         elif kind == "ST":
             cp((("xr",), ("cs",)), ("ao", L * tau, L * tau + L))
         elif kind == "HI":
@@ -382,8 +415,8 @@ def rank_program(g, core, T, topo):
                 send(T.cores[(rank - t) % N], "ho", 32 * tau, 32 * tau + 32, "hn", 32 * tau, "h%d" % tau)
         elif kind == "CO":
             if tau < TAU - 1:
-                mm(("pa", 0, 16), ("one",), ("ho", 32 * tau + 16, 32 * tau + 32))
-                op("v", lambda v: v.tensor_reduce(T.af[:], T.pa[:, 0:16], AxisListType.X, OP.add), [R("pa")], [R("af")])
+                mm(("pa", 256, 272), ("one",), ("ho", 32 * tau + 16, 32 * tau + 32))
+                op("v", lambda v: v.tensor_reduce(T.af[:], T.pa[:, 256:272], AxisListType.X, OP.add), [R("pa")], [R("af")])
                 cp(("ai", 0, 1), ("af",))
                 ts(("ai", 1, 2), ("ai", 0, 1), 63, OP.bitwise_and)
                 ts(("lim",), ("ai", 1, 2), ("thf",), OP.add, 16777216.0, OP.mult)
@@ -396,8 +429,7 @@ def rank_program(g, core, T, topo):
     def spread(p0, p1):
         for a in range(16):
             ts(("ed", p0 * L + a, p1 * L, 16), ("hl", p0 * 16, p1 * 16), ("u16", a, a + 1), OP.mult, tag=("ed%d" % a, p0 * L, p1 * L))
-
-    EDS = [("ed%d" % a, 0, 6 * L) for a in range(16)]
+        need("p", [("ed%d" % a, p0 * L, p1 * L) for a in range(16)], [])
 
     def early_end(gen):
         for t in range(4):
@@ -407,36 +439,37 @@ def rank_program(g, core, T, topo):
                 cp(("er",), (b, o + 16, o + 32))
             else:
                 tt(("er",), ("er",), (b, o + 16, o + 32), OP.add)
-        spread(0, 4)
+        cp(("hl", 64, 80), ("er",))
+        spread(0, 5)
+        mm(("pa", 0, L), ("bo",), ("ed", 4 * L, 5 * L))
+        act(("eb",), ("pa", 0, L), AF.Copy)
         ts(("gm",), ("og",), ("pf", 6, 7), OP.mult)
 
     def registers_and_sums():
         cp(("fo", L, 2 * L), ("ao", L * (TAU - 1), L * TAU))
-        dma(T.ya[:], T.fo[:, L:2 * L], [R("fo", L, 2 * L)], [])
+        dma([(T.ya[:], T.fo[:, L:2 * L])], [R("fo", L, 2 * L)], None, True)
         for h in range(2):
             o = h * (ZC + 1)
             for s in range(16):
                 mm(("pe0", 128 * h, 128 * h + 128), ("ib",), ("xr", o + s, o + ZC, 16), s == 0, s == 15)
         cp(("fo", 2 * L, 3 * L), ("pe0", 0, L))
-        dma(T.ys[:], T.fo[:, 2 * L:3 * L], [R("fo", 2 * L, 3 * L)], [])
+        dma([(T.ys[:], T.fo[:, 2 * L:3 * L])], [R("fo", 2 * L, 3 * L)], None, True)
 
     def end(gen):
         b, o = plane(gen, 4)
-        tt(("hl", 80, 96), ("er",), (b, o + 16, o + 32), OP.add)
-        cp(("hl", 64, 80), (b, o, o + 16))
-        spread(4, 6)
-        need("p", EDS, [])
-        mm(("pa", 0, L), ("bo",), ("ed", 5 * L, 6 * L))
-        for t in range(5):
-            mm(("pb", 0, L), ("ss", t * 128, t * 128 + 128), ("ed", t * L, (t + 1) * L), t == 0, t == 4)
-        ts(("ind",), ("pa", 0, L), ROW, OP.is_equal)
+        tt(("et",), ("eb",), ("nb2",), OP.add)
+        ts(("ind",), ("et",), ROW, OP.is_equal)
         op("v", lambda v: v.tensor_tensor_scan(T.pre[:], T.on[:], T.ind[:], 0.0, OP.mult, OP.add), [R("on"), R("ind")], [R("pre")])
         mm(("pa", 300, 301), ("lt",), ("pre", L - 1, L))
-        tt(("da",), ("pb", 0, L), ("gm",), OP.add)
+        cp(("hl", 64, 80), (b, o, o + 16))
         ts(("x1",), ("pre",), ("pa", 300, 301), OP.add, -1.0, OP.add)
         tt(("x2",), ("x1",), ("ind",), OP.mult)
         for a in range(16):
             mm(("pa", 320, 336), ("ss", a * 128, a * 128 + 128), ("x2", a, L, 16), a == 0, a == 15)
+        spread(4, 5)
+        for t in range(5):
+            mm(("pb", 0, L), ("ss", t * 128, t * 128 + 128), ("ed", t * L, (t + 1) * L), t == 0, t == 4)
+        tt(("da",), ("pb", 0, L), ("gm",), OP.add)
         cp(("pl",), ("pa", 320, 336))
         cp((("sr",), ("pl",)), ("da",))
         ob = K * gen
@@ -451,21 +484,27 @@ def rank_program(g, core, T, topo):
 
     for tau in range(TAU):
         gen, t = divmod(tau, ST)
+        if tau == 0:
+            for tok in FIRST:
+                if tok[0] == "Q":
+                    turn(int(tok[1:]))
+                elif tok == "RT":
+                    turns()
+                elif tok == "LC":
+                    constants()
+                elif tok == "GC":
+                    act(("g16",), ("g4", 0, GW), AF.Copy)
+                else:
+                    run(tok.rstrip("'"), 1 if tok[-1] == "'" else 0)
+            continue
         if t == 0:
             for tok in ORDER:
                 if tok[-1] == "'":
                     run(tok[0:-1], tau)
-                    if tau == 0 and tok == "RR0'":
-                        late_constants()
-        if tau == ST:
             turn_own()
         for tok in ORDER:
             if tok[-1] != "'":
                 run(tok, tau)
-                for n in ROT.get(tok, ()) if tau == 0 else ():
-                    turn(n)
-                if tau == 0 and tok == "X1.0":
-                    later_constants()
             elif t < ST - 1:
                 run(tok[0:-1], tau + 1)
         if t == ST - 1:
@@ -475,7 +514,7 @@ def rank_program(g, core, T, topo):
 
     ts(("fo", 0, L), ("og",), 0.0, OP.is_le, 2047.0, OP.add)
     tt(("fo", 0, L), ("fo", 0, L), ("og",), OP.add)
-    dma(T.yg[:], T.fo[:, 0:L], [R("fo", 0, L)], [])
+    dma([(T.yg[:], T.fo[:, 0:L])], [R("fo", 0, L)], None, True)
     for i in range(nd[0]):
         if known["s"].get("d%d" % i, 0) < 16:
             g.sync.wait_ge(T.sem["d%d" % i], 16)

from concourse.mybir import AluOpType, AxisListType, ActivationFunctionType
OP = AluOpType
AF = ActivationFunctionType
N, GENS, ST, K = 4, 2, 5, 64
L, GW, XW = 256, 2048, 4096
ZC = 2048
XB = XW + 16
MAGIC = 12582913.0
TAU = GENS * ST
CUT = [(0, 128, (64, 64)), (128, 256, (64, 64))]
NCH = len(CUT)
DMAS = 26
ORDER = """D0 NG1 DA0 WW1 OF1 TR0 E1.0 NL1 D1 X0.0 DA1 E1.1 X0.1 TR1 AB0.0 AB0.1 WW0 X1.0 GO0 GV0 PK0 YY0 X1.1 PC0 AB1.0 M10 ML0
 AB1.1 GO1 EE GV1 MC0 PK1 M30 M20 YY1 RR0' PC1 SB0' M11 OF0' ML1 NG0' M21 MC1 M31 ST CO E0.1' E0.0' HI NL0' RR1' SB1'""".split()
FIRST = """LC WW1 RR0 SB0 NG0 OF0 RR1 RT SB1 GC E0.0 E0.1 Q1 Q0 Q3 Q8 Q5 Q2 Q7 WW0 Q10 NL0 OF1 Q11 NG1 D0 DA0 TR0 Q9 E1.0 NL1 D1
 X0.0 X0.1 DA1 TR1 Q6 E1.1 AB0.0 AB0.1 X1.0 GO0 GV0 PK0 X1.1 Q4 PC0 AB1.0 EE M10 AB1.1 GO1 ML0 M30 MC0 YY0 GV1 M20 PK1 YY1
 RR0' PC1 M11 SB0' OF0' ML1 MC1 CO NG0' M31 M21 ST E0.0' E0.1' RR1' SB1' HI NL0'""".split()
ROTA = (0, 2, 3, 4, 8, 10, 11)
TRQ = ["aaggggvvvvvvvvvv", "aagggggggvvvvvvv"]
HFA, YYA = (1, 0), (1, 0)

SCRATCH = {}
for _n, _w, _d in (
        ("gi", GW, "int32"), ("g4", 4 * GW, "float32"), ("n4", 4 * GW, "int32"), ("g16", GW, "float16"), ("xr", XB, "bfloat16"), ("w1", GW, "bfloat16"),
        ("eg", 16 * L, "float16"), ("uu", 16 * L, "float16"), ("ab", 16 * L, "float16"), ("tr", 16 * L, "bfloat16"),
        ("rr", L, "float16"), ("sb", L, "float16"), ("ww", L, "bfloat16"), ("m0", L, "bfloat16"), ("of", L, "uint16"), ("ng", L, "float16"),
        ("nl", 16, "uint16"), ("nf", 16, "float32"), ("dd", L, "bfloat16"), ("tt", L, "bfloat16"), ("xl", L, "uint16"),
        ("ok", L, "bfloat16"), ("ff", L, "float16"), ("qq", 3 * L, "float16"), ("yy", L, "bfloat16"), ("xo", 16, "uint16"), ("ti", 64, "float32"),
        ("yi", 16, "int32"), ("li", 64, "int32"), ("zs", 16, "float32"), ("zr", 16, "float32"), ("zf", 16, "float32"),
        ("lo", 64 * TAU, "uint16"), ("ln", 64 * TAU, "uint16"), ("lc", 64, "uint16"), ("ci", 16, "int32"), ("cs", 16, "uint16"), ("cb", 16, "float32"),
        ("ao", L * TAU, "bfloat16"), ("an", L * TAU, "bfloat16"), ("ho", 32 * TAU, "float16"), ("hn", 32 * TAU, "float16"), ("hl", 80, "float16"), ("er", 16, "float32"),
        ("ed", 5 * L, "float16"), ("eb", L, "float16"), ("nb2", L, "float16"), ("et", L, "float16"),
        ("og", L, "float32"), ("gm", L, "float32"), ("da", L, "float32"), ("sr", L, "float32"), ("rv", L, "float32"),
        ("bi", 2 * K, "float32"), ("o16", L, "float16"), ("ind", L, "float16"), ("pre", L, "float16"), ("on", L, "float16"), ("x1", L, "float16"), ("x2", L, "float16"),
        ("pl", 16, "uint16"), ("pr", 16, "uint16"), ("af", 1, "float32"), ("ai", 2, "int32"), ("lim", 1, "float32"), ("thi", 1, "int32"), ("thf", 1, "float32"),
        ("jj", L, "int32"), ("jf", L, "float32"), ("jt", 128, "int32"), ("kk", 16, "int32"), ("kb", 16, "int32"), ("kf", 16, "float32"), ("wf", 16, "float32"),
        ("pi", 4, "int32"), ("pf", 8, "float32"), ("u16", 16, "float32"), ("tw", 16, "bfloat16"), ("ts", 16, "bfloat16"), ("tm", 16, "bfloat16"),
        ("se", 2048, "float16"), ("ss", 2048, "float16"), ("idn", 128, "float16"), ("ib", 128, "bfloat16"), ("bo", 128, "float16"), ("bh", 128, "bfloat16"), ("bn", 128, "bfloat16"),
        ("lt", 128, "float16"), ("l2", 128, "float16"), ("one", 128, "float16"), ("rt", 384, "float16"), ("r2", 384, "float16"), ("jr", 384, "int32"),
        ("fo", 3 * L, "float32")):
    SCRATCH[_n] = ("sbuf", [128, _w], _d)
PSUM = ["pe0", "pe1", "pd0", "pd1", "pl0", "pl1", "pa", "pb"]
for _n in PSUM:
    SCRATCH[_n] = ("psum", [128, 512], "float32")
SEMAPHORES = ["v", "a", "p", "gc", "loc", "b0", "b1"] + ["d%d" % i for i in range(DMAS)] + ["h%d" % i for i in range(TAU)]
for _b in range(NCH):
    SEMAPHORES += ["li%d_%d" % (_t, _b) for _t in range(TAU)] + ["ar%d_%d" % (_t, _b) for _t in range(TAU)]


def rank_program(g, core, T, topo):
    rank = T.rank_of(core)
    if rank is None:
        return
    queues = {"v": g.vector, "a": g.scalar, "p": g.tensor, "g": g, "s": g.sync}
    own = {"v": "v", "a": "a", "p": "p", "g": "gc"}
    cnt = {"v": 0, "a": 0, "p": 0, "gc": 0}
    known = {q: {} for q in queues}
    clock = {}
    wr, rd = {}, {}
    nd = [0]
    locs = [0]

    def R(name, lo=0, hi=None):
        return (name, lo, SCRATCH[name][1][-1] if hi is None else hi)

    def need(q, reads, writes):
        best = {}

        def look(lists, rs):
            for name, lo, hi in rs:
                ps = name in PSUM
                for l, h, q2, (s, n) in lists.get(name, ()):
                    if (q2 != q if ps else (l < hi and lo < h)) and n > known[q].get(s, 0) and n > best.get(s, 0):
                        best[s] = n
        look(wr, reads + writes)
        look(rd, writes + [r for r in reads if r[0] in PSUM])
        for s in sorted(best):
            n = best[s]
            if n > known[q].get(s, 0):
                queues[q].wait_ge(T.sem[s], n)
                known[q][s] = n
                for s2, n2 in clock.get((s, n), {}).items():
                    if n2 > known[q].get(s2, 0):
                        known[q][s2] = n2

    def note(q, reads, writes, tok):
        for name, lo, hi in writes:
            for d in (wr, rd):
                d[name] = [e for e in d.get(name, ()) if not (lo <= e[0] and e[1] <= hi)]
            wr[name].append((lo, hi, q, tok))
        for name, lo, hi in reads:
            rd[name] = [e for e in rd.get(name, ()) if not (lo <= e[0] and e[1] <= hi and e[2] == q)] + [(lo, hi, q, tok)]

    def op(q, fn, reads, writes):
        need(q, reads, writes)
        s = own[q]
        fn(queues[q]).then_inc(T.sem[s], 1)
        cnt[s] += 1
        clock[(s, cnt[s])] = dict(known[q])
        note(q, reads, writes, (s, cnt[s]))

    def dma(pairs, reads, reg, out=False):
        need("s", reads, [] if out else [reg])
        toks = []
        for o, src in pairs:
            s = "d%d" % nd[0]
            nd[0] += 1
            g.sync.dma_start(o, src).then_inc(T.sem[s], 16)
            clock[(s, 16)] = dict(known["s"])
            toks.append((s, (s, 16)))
        for s, tok in toks:
            if len(pairs) > 1:
                wr[reg[0]] = list(wr.get(reg[0], ())) + [reg[1:3] + (s, tok)]
            else:
                note(s, reads, [] if out else [reg], tok)

    def send(dst, name, lo, hi, to, lo2, sem):
        need("g", [(name, lo, hi)], [])
        rid, pid, _ = topo.addr(dst)
        ne = len(topo.engines(core, dst))
        g.remote_dma(T[to][:, lo2:lo2 + hi - lo], T[name][:, lo:hi], T.sem[sem], T.sem.loc, pid, rid, topo.mask(core, dst))
        locs[0] += ne
        note(sem, [], [(to, lo2, lo2 + hi - lo)], (sem, ne))

    def X(r):
        if len(r) == 1:
            return T[r[0]][:], R(r[0])
        if len(r) == 4:
            return T[r[0]][:, r[1]:r[2]:r[3]], r[0:3]
        return T[r[0]][:, r[1]:r[2]], r

    def side(r):
        if len(r) == 2 and isinstance(r[0], tuple):
            return X(r[0])[0].indirect(X(r[1])[0]), [X(r[0])[1], X(r[1])[1]]
        a, i = X(r)
        return a, [i]

    def sc(s):
        return (X(s)[0], [X(s)[1]]) if isinstance(s, tuple) else (s, [])

    def ts(out, src, s1, op0, s2=None, op1=None, tag=None):
        o, io = side(out)
        a, ia = side(src)
        c1, i1 = sc(s1)
        c2, i2 = sc(s2)
        w = [tag] if tag else io
        if op1 is None:
            op("v", lambda v: v.tensor_scalar(o, a, c1, None, op0), ia + i1, w)
        else:
            op("v", lambda v: v.tensor_scalar(o, a, c1, c2, op0, op1), ia + i1 + i2, w)

    def tt(out, a, b, op0, more=()):
        o, io = side(out)
        x, ix = side(a)
        y, iy = side(b)
        op("v", lambda v: v.tensor_tensor(o, x, y, op0), ix + iy + list(more), io)

    def cp(out, src, tag=None):
        o, io = side(out)
        a, ia = side(src)
        op("v", lambda v: v.tensor_copy(o, a), ia + (io[1:] if len(io) > 1 else []), [tag] if tag else io[:1])

    def act(out, src, f, bias=0.0, scale=1.0, tag=None):
        o, io = side(out)
        a, ia = side(src)
        b, ib = sc(bias)
        c, ic = sc(scale)
        op("a", lambda s: s.activation(o, a, f, bias=b, scale=c), ia + ib + ic, [tag] if tag else io)

    def sel(out, src, pattern, cmp, base, ch, tag=None):
        o, io = side(out)
        a, ia = side(src)
        op("g", lambda q: q.affine_select(o, a, pattern, cmp, 0.0, base, ch), ia, [tag] if tag else io)

    def iota(out, pattern, base, ch):
        o, io = side(out)
        op("g", lambda q: q.iota(o, pattern, base, ch), [], io)

    def fill(out, c):
        o, io = side(out)
        op("v", lambda v: v.memset(o, c), [], io)

    def mm(out, lhsT, rhs, start=True, stop=True):
        o, io = side(out)
        a, ia = side(lhsT)
        b, ib = side(rhs)
        op("p", lambda t: t.matmul(o, a, b, start, stop), ia + ib, io)

    nxt = T.cores[(rank + 1) % N]

    H = GW // 2
    for lo in (0, H):
        dma([(T.gi[:, lo:lo + H], T.gn[:, lo:lo + H])], [], R("gi", lo, lo + H))
    dma([(T.n4[:, 0:GW], T.nb[:])], [], R("n4", 0, GW))
    dma([(T.thi[:], T.th[:])], [], R("thi"))
    dma([(T.an[:, 0:L], T.a0[:])], [], R("an", 0, L))
    dma([(T.xr[:, 0:ZC], T.x[:, 0:ZC])], [], R("xr", 0, ZC))
    iota(("pi", 0, 1), [[0, 1]], 0, 1)
    iota(("jj",), [[1, L]], 0, 0)
    iota(("kk",), [[0, 4], [-1, 4]], 16, 1)
    fill(("w1",), 1.0)
    fill(("xr", ZC, XB), 0.0)
    dma([(T.xr[:, ZC + 1:XW + 1], T.x[:, ZC:XW])], [], R("xr", ZC, XB))
    for k in range(1, 4):
        reg = R("n4", k * GW, (k + 1) * GW)
        dma([(T.n4[k:128, reg[1]:reg[2]], T.nb[0:128 - k, :])], [], reg)
        rows = [(T.n4[u::16, reg[1]:reg[2]], T.nb[16 - k + u::16, :]) for u in range(k)]
        dma(rows, [], reg)
    sel(("ss",), ("w1",), [[16384, 16], [-16, 8], [-16384, 16]], OP.is_ge, 0, 1)
    sel(("ss",), ("ss",), [[-16384, 16], [16, 8], [16384, 16]], OP.is_ge, 15, -1)
    sel(("se",), ("w1",), [[-1024, 16], [16, 8], [1025, 16]], OP.is_equal, 0, -1)
    iota(("jr",), [[4, 3], [32, 8], [1, 16]], 4, 0)
    ts(("pi", 1, 2), ("pi", 0, 1), 15, OP.bitwise_and)
    ts(("pi", 2, 3), ("pi", 0, 1), 4, OP.arith_shift_right)
    cp(("pf", 0, 3), ("pi", 0, 3))
    ROW, GRP = ("pf", 1, 2), ("pf", 2, 3)
    cp(("jf",), ("jj",))
    ts(("idn",), ("jf", 0, 128), ("pf", 0, 1), OP.is_equal)
    ts(("jt",), ("jj", 0, 128), 4, OP.arith_shift_right)
    ts(("bo",), ("jt",), GRP, OP.is_equal)
    ts(("u16",), ("jf", 0, 16), ROW, OP.is_equal)
    ts(("pf", 3, 4), ROW, 8.0, OP.mult)
    ts(("pf", 4, 5), ROW, 16.0, OP.mult)
    ts(("pf", 5, 6), ROW, 1.0, OP.add, 2048.0, OP.mult)
    ts(("pf", 6, 7), ROW, 5.0, OP.is_ge)
    ts(("pf", 7, 8), GRP, 16.0, OP.mult, ("pf", 0, 1), OP.add)
    ts(("zf",), ("jf", 0, 16), 128.0, OP.mult, ("pf", 3, 4), OP.add)
    cp(("lc", 0, 16), ("zf",))
    ts(("lc", 16, 32), ("zf",), 0.0, OP.mult)
    ts(("kb",), ("jj", 0, 16), 2, OP.arith_shift_right)
    ts(("ts",), ("kb",), 2048.0, OP.mult)
    cp(("tm",), ("u16",))
    for lo in (0, H):
        ts(("g4", lo, lo + H), ("gi", lo, lo + H), 1.0 + 2.0 ** -12, OP.mult, MAGIC, OP.add)
        act(("g4", lo, lo + H), ("g4", lo, lo + H), AF.Copy, bias=-(MAGIC + 2048.0))

    def constants():
        ts(("kk",), ("kk",), 15, OP.bitwise_and)
        fill(("wf",), 16777216.0)
        for j in range(4):
            ts(("kb",), ("kk",), j, OP.arith_shift_right, 1, OP.bitwise_and)
            ts(("kf",), ("kb",), 2.0 ** -(1 << j) - 1.0, OP.mult, 1.0, OP.add)
            tt(("wf",), ("wf",), ("kf",), OP.mult)
        cp(("tw",), ("wf",))
        ts(("bh",), ("bo",), 0.5, OP.mult)
        ts(("bn",), ("bo",), -0.5, OP.mult)
        cp(("ib",), ("idn",))
        ts(("cb",), ("jf", 0, 16), 256.0, OP.mult, ("pf", 4, 5), OP.add)
        ts(("cb", 8, 16), ("cb", 8, 16), 1.0, OP.add)
        cp(("one",), ("w1", 0, 128))
        cp(("on",), ("w1", 0, L))
        ts(("jt",), ("jj", 0, 128), 15, OP.bitwise_and)
        ts(("l2",), ("jt",), ROW, OP.is_gt)
        tt(("lt",), ("l2",), ("bo",), OP.mult)
        ts(("thf",), ("thi",), 1.0, OP.add)
        ts(("lim",), ("thf",), 16777216.0, OP.mult)
        cp(("og",), ("g4", 0, GW, 8))

    def turns():
        ts(("rt",), ("jr",), ("pf", 7, 8), OP.is_equal)
        ts(("r2",), ("jr",), -16.0, OP.add, ("pf", 7, 8), OP.is_equal)
        tt(("rt",), ("rt",), ("r2",), OP.add)

    def turn(n):
        s, lo = 1 + n // 4, 512 * (n % 4)
        bank = ("pa", "pd1")[n % 2]
        mm((bank,), ("rt", (s - 1) * 128, s * 128), ("g16", lo, lo + 512))
        out = ("g4", s * GW + lo, s * GW + lo + 512)
        if n in ROTA:
            act(out, (bank,), AF.Copy)
        else:
            cp(out, (bank,))

    def turn_own():
        cp(("o16",), ("og",))
        for s in range(1, 4):
            bank = ("pa", "pd1")[s % 2]
            mm((bank, 0, L), ("rt", (s - 1) * 128, s * 128), ("o16",))
            if s == 2:
                act(("g4", s * GW, (s + 1) * GW, 8), (bank, 0, L), AF.Copy)
            else:
                cp(("g4", s * GW, (s + 1) * GW, 8), (bank, 0, L))

    def lst(tau, b, kind):
        c0, c1 = CUT[b][0:2]
        n = (c1 - c0) // 16
        if tau % ST == 0:
            lo = (0 if kind in (1, 3) else 16) + c0 // 16
            return ("lc", lo, lo + n)
        lo = 64 * tau + c0 // 4 + kind * n
        return ("ln", lo, lo + n)

    def run(tok, tau):
        gen, t = divmod(tau, ST)
        tok, _, js = tok.partition(".")
        kind = tok.rstrip("0123456789") if tok[0] != "M" else tok[0:2]
        b = int(tok[len(kind):]) if tok[len(kind):] else 0
        c0, c1, subs = CUT[b]
        n = c1 - c0
        l0, l1 = c0 // 16, c1 // 16
        lc = l1 - l0
        pe, pd, pn = "pe%d" % (b % 2), "pd%d" % (b % 2), "pl%d" % (b % 2)
        gw = GW if t == 0 else 4 * GW
        e0 = c0 + sum(subs[0:int(js)]) if js else 0
        e1 = e0 + subs[int(js)] if js else 0
        q = 3 * c0
        sco = (pd, 256 + c0, 256 + c1)
        le, lr, ls = [(pn, 64 + k * lc, 64 + (k + 1) * lc) for k in range(3)]
        hv = ("ho", 32 * tau + l0, 32 * tau + l1)
        hf = ("ho", 32 * tau + 16 + l0, 32 * tau + 16 + l1)
        li = [("li", c0 // 4 + k * lc, c0 // 4 + (k + 1) * lc) for k in range(4)]
        yi = ("yi", l0, l1)
        ti = [("ti", 16 * k + l0, 16 * k + l1) for k in range(4)]
        if kind == "RR":
            cp(("rr", c0, c1), (("n4", 0, gw), lst(tau, b, 1)))
        elif kind == "SB":
            act(("sb", c0, c1), (("ts", 0, 16), lst(tau, b, 2)), AF.Copy)
            mm(("pb", c0, c1), ("idn",), ("rr", c0, c1), True, False)
            mm(("pb", c0, c1), ("idn",), ("sb", c0, c1), False, True)
            mm(("pb", 256 + c0, 256 + c1), ("idn",), ("rr", c0, c1))
            act(("m0", c0, c1), (("tm", 0, 16), lst(tau, b, 2)), AF.Copy)
        elif kind == "OF":
            cp(("of", c0, c1), ("pb", c0, c1))
        elif kind == "NG":
            tt(("ng", c0, c1), (("g4", 0, GW), lst(tau, b, 3)), ("m0", c0, c1), OP.mult)
            for a in range(16):
                mm((pn, 0, lc), ("ss", a * 128, a * 128 + 128), ("ng", c0 + a, c1, 16), a == 0, a == 15)
        elif kind == "NL":
            ts(("nl", l0, l1), (pn, 0, lc), 2048.0, OP.add)
            act(("nf", l0, l1), (pn, 0, lc), AF.Copy)
        elif kind == "WW":
            act(("ww", c0, c1), (("tw", 0, 16), lst(tau, b, 2)), AF.Copy)
            ts(("zr", l0, l1), lst(tau, b, 1), 2048.0, OP.add)
            cp(("zs", l0, l1), lst(tau, b, 0))
        elif kind == "E":
            act(("eg", 16 * e0, 16 * e1), (("g4", 0, gw), ("of", e0, e1)), AF.Copy)
            for s in range(16):
                mm((pe, e0, e1), ("se", s * 128, s * 128 + 128), ("eg", 16 * e0 + s, 16 * e1, 16), s == 0, s == 15)
        elif kind == "D":
            an, ao = ("an", L * tau) if t or tau == 0 else ("ao", L * (tau - 1))
            tt(("dd", c0, c1), (("xr",), ("nl", l0, l1)), (an, ao + c0, ao + c1), OP.subtract)
        elif kind == "DA":
            act(("tt", c0, c1), ("dd", c0, c1), AF.Abs)
        elif kind == "TR":
            for s, w in enumerate(TRQ[b]):
                o, tag = ("tr", 16 * c0 + s, 16 * c1, 16), ("tr%d" % s, c0, c1)
                if w == "a":
                    act(o, ("tt", c0, c1), AF.Copy, tag=tag)
                elif w == "g":
                    sel(o, ("tt", c0, c1), [[0, n]], OP.is_ge, 0, 0, tag=tag)
                else:
                    cp(o, ("tt", c0, c1), tag=tag)
        elif kind == "X":
            ts(("xl", e0, e1), (pe, e0, e1), 2048.0, OP.add)
            tt(("uu", 16 * e0, 16 * e1), (("xr",), ("xl", e0, e1)), ("tr", 16 * e0, 16 * e1), OP.add, more=[("tr%d" % s, e0, e1) for s in range(16)])
        elif kind == "AB":
            act(("ab", 16 * e0, 16 * e1), ("uu", 16 * e0, 16 * e1), AF.Abs, bias=-255.0)
            for s in range(16):
                mm((pd, e0, e1), ("ss", s * 128, s * 128 + 128), ("ab", 16 * e0 + s, 16 * e1, 16), s == 0, s == 15)
        elif kind == "GO":
            act((pd, c0, c1), (pd, c0, c1), AF.Relu, bias=("lim",), scale=-16777216.0)
        elif kind == "GV":
            tt(("ok", c0, c1), (pd, c0, c1), ("ww", c0, c1), OP.min)
            mm(sco, ("bh",), ("ok", c0, c1))
        elif kind == "PK":
            tt(("ff", c0, c1), ("ok", c0, c1), sco, OP.is_gt)
            tt(("qq", q, q + n), ("ff", c0, c1), (pe, c0, c1), OP.mult)
            tt(("qq", q + n, q + 2 * n), ("ff", c0, c1), ("pb", 256 + c0, 256 + c1), OP.mult)
            act(("qq", q + 2 * n, q + 3 * n), ("ff", c0, c1), AF.Copy, scale=("pf", 5, 6))
        elif kind == "PC":
            for a in range(16):
                mm((pn, 64, 64 + 3 * lc), ("ss", a * 128, a * 128 + 128), ("qq", q + a, q + 3 * n, 16), a == 0, a == 15)
        elif kind == "YY":
            if t == ST - 1:
                act(("nb2", c0, c1), sco, AF.Relu, bias=1.0, scale=-1.0)
            if YYA[b]:
                mm((pn, 384, 384 + n), ("ib",), ("tt", c0, c1), True, False)
                mm((pn, 384, 384 + n), ("bn",), ("ok", c0, c1), False, True)
                act(("yy", c0, c1), (pn, 384, 384 + n), AF.Relu)
            else:
                tt(("yy", c0, c1), ("tt", c0, c1), sco, OP.subtract)
        elif kind == "M1":
            if HFA[b]:
                act(hf, ls, AF.Relu, bias=1.0, scale=-1.0)
            else:
                ts(hf, ls, 0.0, OP.is_equal)
            ts(("xo", l0, l1), le, 2048.0, OP.add)
            tt(ti[0], ls, ("zs", l0, l1), OP.add)
            tt(ti[1], hf, ("zr", l0, l1), OP.mult)
            tt(ti[2], lr, ti[1], OP.add)
            tt(yi, ti[0], ti[2], OP.add)
            ts(li[2], yi, 11, OP.arith_shift_right, 15, OP.bitwise_and)
        elif kind == "ML":
            if t < ST - 1:
                for k, m in ((1, 8191), (3, 2047), (0, 24576)):
                    ts(li[k], yi, m, OP.bitwise_and)
                o = 64 * tau + c0 // 4
                cp(("lo", o, o + 4 * lc), ("li", c0 // 4, c0 // 4 + 4 * lc))
                send(nxt, "lo", o, o + 4 * lc, "ln", o + 64, "li%d_%d" % (tau, b))
        elif kind == "M2":
            ao = L * tau
            tt(("ao", ao + c0, ao + c1), (("xr",), ("xo", l0, l1)), ("yy", c0, c1), OP.max)
            if t < ST - 1:
                send(nxt, "ao", ao + c0, ao + c1, "an", ao + L + c0, "ar%d_%d" % (tau, b))
        elif kind == "MC":
            tt(("ci", l0, l1), li[2], ("cb", l0, l1), OP.add)
            cp(("cs", l0, l1), ("ci", l0, l1))
        elif kind == "M3":
            tt(ti[3], hf, ("nf", l0, l1), OP.mult)
            tt(hv, le, ti[3], OP.add)
        elif kind == "ST":
            cp((("xr",), ("cs",)), ("ao", L * tau, L * tau + L))
        elif kind == "HI":
            if t in (1, 2, 3):
                send(T.cores[(rank - t) % N], "ho", 32 * tau, 32 * tau + 32, "hn", 32 * tau, "h%d" % tau)
        elif kind == "CO":
            if tau < TAU - 1:
                mm(("pa", 256, 272), ("one",), ("ho", 32 * tau + 16, 32 * tau + 32))
                op("v", lambda v: v.tensor_reduce(T.af[:], T.pa[:, 256:272], AxisListType.X, OP.add), [R("pa")], [R("af")])
                cp(("ai", 0, 1), ("af",))
                ts(("ai", 1, 2), ("ai", 0, 1), 63, OP.bitwise_and)
                ts(("lim",), ("ai", 1, 2), ("thf",), OP.add, 16777216.0, OP.mult)
        elif kind == "EE" and t == ST - 1:
            early_end(gen)

    def plane(gen, t):
        return "hn" if t in (1, 2, 3) else "ho", 32 * (ST * gen + t)

    def spread(p0, p1):
        for a in range(16):
            ts(("ed", p0 * L + a, p1 * L, 16), ("hl", p0 * 16, p1 * 16), ("u16", a, a + 1), OP.mult, tag=("ed%d" % a, p0 * L, p1 * L))
        need("p", [("ed%d" % a, p0 * L, p1 * L) for a in range(16)], [])

    def early_end(gen):
        for t in range(4):
            b, o = plane(gen, t)
            cp(("hl", 16 * t, 16 * t + 16), (b, o, o + 16))
            if t == 0:
                cp(("er",), (b, o + 16, o + 32))
            else:
                tt(("er",), ("er",), (b, o + 16, o + 32), OP.add)
        cp(("hl", 64, 80), ("er",))
        spread(0, 5)
        mm(("pa", 0, L), ("bo",), ("ed", 4 * L, 5 * L))
        act(("eb",), ("pa", 0, L), AF.Copy)
        ts(("gm",), ("og",), ("pf", 6, 7), OP.mult)

    def registers_and_sums():
        cp(("fo", L, 2 * L), ("ao", L * (TAU - 1), L * TAU))
        dma([(T.ya[:], T.fo[:, L:2 * L])], [R("fo", L, 2 * L)], None, True)
        for h in range(2):
            o = h * (ZC + 1)
            for s in range(16):
                mm(("pe0", 128 * h, 128 * h + 128), ("ib",), ("xr", o + s, o + ZC, 16), s == 0, s == 15)
        cp(("fo", 2 * L, 3 * L), ("pe0", 0, L))
        dma([(T.ys[:], T.fo[:, 2 * L:3 * L])], [R("fo", 2 * L, 3 * L)], None, True)

    def end(gen):
        b, o = plane(gen, 4)
        tt(("et",), ("eb",), ("nb2",), OP.add)
        ts(("ind",), ("et",), ROW, OP.is_equal)
        op("v", lambda v: v.tensor_tensor_scan(T.pre[:], T.on[:], T.ind[:], 0.0, OP.mult, OP.add), [R("on"), R("ind")], [R("pre")])
        mm(("pa", 300, 301), ("lt",), ("pre", L - 1, L))
        cp(("hl", 64, 80), (b, o, o + 16))
        ts(("x1",), ("pre",), ("pa", 300, 301), OP.add, -1.0, OP.add)
        tt(("x2",), ("x1",), ("ind",), OP.mult)
        for a in range(16):
            mm(("pa", 320, 336), ("ss", a * 128, a * 128 + 128), ("x2", a, L, 16), a == 0, a == 15)
        spread(4, 5)
        for t in range(5):
            mm(("pb", 0, L), ("ss", t * 128, t * 128 + 128), ("ed", t * L, (t + 1) * L), t == 0, t == 4)
        tt(("da",), ("pb", 0, L), ("gm",), OP.add)
        cp(("pl",), ("pa", 320, 336))
        cp((("sr",), ("pl",)), ("da",))
        ob = K * gen
        send(nxt, "sr", 0, K, "bi", ob, "b%d" % gen)
        ts(("pr",), ("pa", 320, 336), -1.0, OP.mult, 255.0, OP.add)
        cp((("rv",), ("pr",)), ("og",))
        cp(("rv", 0, K, 2), ("sr", 0, K, 2))
        if gen == GENS - 1:
            registers_and_sums()
        cp(("rv", 1, K, 2), ("bi", ob + 1, ob + K, 2))
        cp(("og",), (("rv",), ("pr",)))

    for tau in range(TAU):
        gen, t = divmod(tau, ST)
        if tau == 0:
            for tok in FIRST:
                if tok[0] == "Q":
                    turn(int(tok[1:]))
                elif tok == "RT":
                    turns()
                elif tok == "LC":
                    constants()
                elif tok == "GC":
                    act(("g16",), ("g4", 0, GW), AF.Copy)
                else:
                    run(tok.rstrip("'"), 1 if tok[-1] == "'" else 0)
            continue
        if t == 0:
            for tok in ORDER:
                if tok[-1] == "'":
                    run(tok[0:-1], tau)
            turn_own()
        for tok in ORDER:
            if tok[-1] != "'":
                run(tok, tau)
            elif t < ST - 1:
                run(tok[0:-1], tau + 1)
        if t == ST - 1:
            end(gen)
            if gen < GENS - 1:
                cp(("g4", 0, GW, 8), ("og",))

    ts(("fo", 0, L), ("og",), 0.0, OP.is_le, 2047.0, OP.add)
    tt(("fo", 0, L), ("fo", 0, L), ("og",), OP.add)
    dma([(T.yg[:], T.fo[:, 0:L])], [R("fo", 0, L)], None, True)
    for i in range(nd[0]):
        if known["s"].get("d%d" % i, 0) < 16:
            g.sync.wait_ge(T.sem["d%d" % i], 16)
    g.wait_ge(T.sem.loc, locs[0])
    for s in ("v", "a", "p", "gc"):
        g.sync.wait_ge(T.sem[s], cnt[s])
